import numpy as np
import ml_dtypes


def mxq(x, axis, fmt="e4m3"):
    dtype, down = {"e4m3": (ml_dtypes.float8_e4m3fn, 7), "e5m2": (ml_dtypes.float8_e5m2, 14)}[fmt]
    v = np.moveaxis(np.asarray(x, np.float32).astype(ml_dtypes.bfloat16).astype(np.float64), axis, -1)
    blocks = v.reshape(v.shape[:-1] + (-1, 32))
    amax = np.abs(blocks).max(-1, keepdims=True)
    byte = np.maximum(np.where(amax > 0, np.frexp(amax)[1] - 1 + 127, 0) - down, 1)
    scale = np.exp2(byte - 127.0)
    codes = (blocks / scale).astype(np.float32).astype(dtype).astype(np.float64)
    return np.moveaxis((codes * scale).reshape(v.shape), -1, axis)


WIDE = False


def mx_kscale(k):
    if not WIDE:
        return np.ones(k)
    levels = np.array([10, -10, 5, -5, 0])
    if k % 512:
        return np.exp2(np.random.permutation(np.resize(levels, k // 32))).repeat(32)
    a = np.empty((k // 512, 16))
    for p in range(k // 512):
        a[p, :8] = np.random.permutation(np.resize(levels, 8))
        for g in range(8):
            far = levels[np.abs(levels - a[p, g]) >= 10]
            a[p, g + 8] = far[np.random.randint(len(far))]
    return np.exp2(a.ravel()).repeat(32)


def f64(x):
    return np.asarray(x).astype(np.float64)


def striped(idx):
    return np.tile(idx.reshape(-1, 16).T, (8, 1)).astype(np.uint16)


def unstriped(offs):
    return offs[:16].T.reshape(-1).astype(np.int64)


E2M1 = np.array([0.0, 0.5, 1.0, 1.5, 2.0, 3.0, 4.0, 6.0, -0.0, -0.5, -1.0, -1.5, -2.0, -3.0, -4.0, -6.0])


def pack_weight(w, fmt):
    k, n = w.shape
    w = f64(np.asarray(w, np.float32).astype(ml_dtypes.bfloat16)).reshape(k // 32, 32, n)
    amax = np.abs(w).max(1)
    if fmt == "e4m3":
        byte = np.frexp(amax)[1] - 1 + 127 - 7
    else:
        mant, ex = np.frexp(amax / 6.0)
        byte = np.where(mant > 0.5, ex, ex - 1) + 127
    byte = np.clip(np.where(amax > 0, byte, 1), 1, 254)
    scaled = (w * np.exp2(127.0 - byte)[:, None, :]).reshape(k, n).astype(np.float32)
    by_word = np.ascontiguousarray(scaled.reshape(k // 512, 128, 4, n).transpose(0, 1, 3, 2))
    if fmt == "e4m3":
        words = by_word.astype(ml_dtypes.float8_e4m3fn).view(np.uint8)
    else:
        c = by_word.astype(ml_dtypes.float4_e2m1fn).view(np.uint8) & 0xF
        words = (c[..., 0::2] | (c[..., 1::2] << 4)).reshape(k // 512, 128, 2 * n)
    return np.ascontiguousarray(words), np.ascontiguousarray(byte.astype(np.uint8).reshape(k // 512, 16, n))


def unpack_weight(words, scales, fmt):
    g, _, n = scales.shape
    words = np.ascontiguousarray(words).reshape(g, 128, n, -1)
    if fmt == "e4m3":
        vals = words.view(ml_dtypes.float8_e4m3fn).astype(np.float64)
    else:
        nib = np.empty((g, 128, n, 4), np.uint8)
        nib[..., 0::2] = words & 0xF
        nib[..., 1::2] = words >> 4
        vals = E2M1[nib]
    vals = vals * np.repeat(np.exp2(scales.astype(np.float64) - 127.0), 8, axis=1)[..., None]
    return vals.transpose(0, 1, 3, 2).reshape(g * 512, n)


def gelu(v):
    return 0.5 * v * (1.0 + np.tanh(np.sqrt(2.0 / np.pi) * (v + 0.044715 * v**3)))


K, T, E, C, H, N, HOT = 512, 1280, 10, 256, 512, 256, 2


def by_expert(wq, xq):
    return np.concatenate([wq[e].T @ xq[:, e * C:(e + 1) * C] for e in range(E)], axis=1)


def setup_inputs():
    n = np.random.standard_normal
    s = mx_kscale(K)
    u = mx_kscale(H)
    slot_token = np.concatenate([np.random.permutation(T)[:C] for e in range(E)])
    x = pack_weight(n((K, T)) * s[:, None], "e4m3")
    w1h = [pack_weight(m, "e4m3") for m in n((HOT, K, H)) / np.sqrt(K) / s[None, :, None] * u]
    w2h = [pack_weight(m, "e4m3") for m in n((HOT, H, N)) / np.sqrt(H) / u[None, :, None]]
    w1c = [pack_weight(m, "e2m1") for m in n((E - HOT, K, H)) / np.sqrt(K) / s[None, :, None] * u]
    w2c = [pack_weight(m, "e2m1") for m in n((E - HOT, H, N)) / np.sqrt(H) / u[None, :, None]]
    return {
        "x_words": x[0],
        "x_scales": x[1],
        "w1h_words": np.stack([m[0] for m in w1h]),
        "w1h_scales": np.stack([m[1] for m in w1h]),
        "w2h_words": np.stack([m[0] for m in w2h]),
        "w2h_scales": np.stack([m[1] for m in w2h]),
        "w1c_words": np.stack([m[0] for m in w1c]),
        "w1c_scales": np.stack([m[1] for m in w1c]),
        "w2c_words": np.stack([m[0] for m in w2c]),
        "w2c_scales": np.stack([m[1] for m in w2c]),
        "offs": striped(slot_token),
    }


def reference(x_words, x_scales, w1h_words, w1h_scales, w2h_words, w2h_scales, w1c_words, w1c_scales, w2c_words, w2c_scales, offs):
    w1h = np.stack([unpack_weight(w1h_words[e], w1h_scales[e], "e4m3") for e in range(HOT)])
    w2h = np.stack([unpack_weight(w2h_words[e], w2h_scales[e], "e4m3") for e in range(HOT)])
    w1c = np.stack([unpack_weight(w1c_words[e], w1c_scales[e], "e2m1") for e in range(E - HOT)])
    w2c = np.stack([unpack_weight(w2c_words[e], w2c_scales[e], "e2m1") for e in range(E - HOT)])
    idx = unstriped(offs)
    xq = unpack_weight(x_words, x_scales, "e4m3")[:, idx]
    w1 = [*w1h, *w1c]
    w2 = [*w2h, *w2c]
    h = gelu(by_expert(w1, xq))
    y = by_expert(w2, mxq(h, 0, "e4m3"))
    out = y
    return out

@@ -1,0 +1,172 @@
+from contextlib import ExitStack
+
+import concourse.mybir as mybir
+
+K, T, E, C, H, N, HOT = 512, 1280, 10, 256, 512, 256, 2
+COLD = E - HOT
+FLOPS = 2 * E * C * (K * H + H * N)
+
+F32 = mybir.dt.float32
+BF16 = mybir.dt.bfloat16
+I32 = mybir.dt.int32
+U32 = mybir.dt.uint32
+U16 = mybir.dt.uint16
+U8 = mybir.dt.uint8
+FP8X4 = mybir.dt.float8_e4m3fn_x4
+FP4X4 = mybir.dt.float4_e2m1fn_x4
+GELU = mybir.ActivationFunctionType.Gelu_apprx_tanh
+
+P = 128
+PACK = 4
+HALF = 128
+ORDER = [2, 3, 4, 5, 6, 7, 8, 9, 0, 1]
+LAG = 2
+
+
+def tile_moe_hot_s_mlp_gelu_kernel(
+    tc, x_words, x_scales, w1h_words, w1h_scales, w2h_words, w2h_scales,
+    w1c_words, w1c_scales, w2c_words, w2c_scales, offs, out,
+):
+    nc = tc.nc
+    with ExitStack() as ctx:
+        held = ctx.enter_context(tc.tile_pool(name="held", bufs=1))
+        work = ctx.enter_context(tc.tile_pool(name="work", bufs=4))
+        psum1 = ctx.enter_context(tc.psum_pool(name="psum1", bufs=6))
+        psum2 = ctx.enter_context(tc.psum_pool(name="psum2", bufs=2))
+
+        offsets = held.tile([P, E * C // 16], U16, name="offsets")
+        xw = held.tile([P, T], U32, name="xw", align_bytes=64)
+        xs = held.tile([P, T], U8, name="xs", align_bytes=64)
+        w1c_first = held.tile([P, 2, 2 * H], U8, name="w1c_first", align_bytes=64)
+        w1c_rest = held.tile([P, COLD - 2, 2 * H], U8, name="w1c_rest", align_bytes=64)
+        w1h = held.tile([P, HOT, H], I32, name="w1h", align_bytes=64)
+        w2c = held.tile([P, COLD, 2 * N], U8, name="w2c", align_bytes=64)
+        w2h = held.tile([P, HOT, N], I32, name="w2h", align_bytes=64)
+        s1c = held.tile([P, COLD, H], U8, name="s1c", align_bytes=64)
+        s2c = held.tile([P, COLD, N], U8, name="s2c", align_bytes=64)
+        s1h = held.tile([P, H], U8, name="s1h", align_bytes=64)
+        s2h = held.tile([P, N], U8, name="s2h", align_bytes=64)
+        s1h_perm = held.tile([P, H], U8, name="s1h_perm", align_bytes=64)
+        warm = held.tile([P, 16], F32, name="warm")
+        warm_out = held.tile([P, 16], BF16, name="warm_out")
+
+        nc.vector.memset(s1c[:].rearrange("p e n -> p (e n)").bitcast(I32), 0)
+        nc.gpsimd.memset(xs[:].bitcast(I32), 0)
+        nc.vector.memset(s2c[:].rearrange("p e n -> p (e n)").bitcast(I32), 0)
+        nc.vector.memset(s1h[:].bitcast(I32), 0)
+        nc.vector.memset(s2h[:].bitcast(I32), 0)
+        nc.gpsimd.memset(warm[:], 0.0)
+        nc.scalar.activation(warm_out[:], warm[:], GELU)
+
+        def load_cold_words(tile, words):
+            nc.sync.dma_start(tile[:].bitcast(I32), words.rearrange("e s p b -> p (e s) b").bitcast(I32))
+
+        def load_hot_words(tile, words):
+            nc.sync.dma_start(tile[:], words.rearrange("e s p n d -> p (e s) (n d)").bitcast(I32))
+
+        def load_cold_scales(tile, scales):
+            for q in range(4):
+                nc.sync.dma_start(
+                    tile[32 * q : 32 * q + 4, :, :].bitcast(I32),
+                    scales[:, 0, 4 * q : 4 * q + 4, :].rearrange("e r n -> r e n").bitcast(I32),
+                )
+
+        def load_hot_scales(tile, scales):
+            for q in range(4):
+                nc.sync.dma_start(
+                    tile[32 * q : 32 * q + 4 * HOT, :].bitcast(I32),
+                    scales[:, 0, 4 * q : 4 * q + 4, :].bitcast(I32),
+                )
+
+        nc.sync.dma_start(offsets[:], offs)
+        nc.sync.dma_start(xw[:].bitcast(I32), x_words[0].rearrange("p t d -> p (t d)").bitcast(I32))
+        load_cold_words(w1c_first, w1c_words[0:2])
+        load_cold_scales(s1c, w1c_scales)
+        for q in range(4):
+            nc.sync.dma_start(
+                xs[32 * q : 32 * q + 4, :].bitcast(I32), x_scales[0, 4 * q : 4 * q + 4, :].bitcast(I32)
+            )
+        load_cold_words(w1c_rest, w1c_words[2:COLD])
+        load_cold_scales(s2c, w2c_scales)
+        load_cold_words(w2c, w2c_words)
+        load_hot_words(w1h, w1h_words)
+        load_hot_scales(s1h, w1h_scales)
+        load_hot_words(w2h, w2h_words)
+        load_hot_scales(s2h, w2h_scales)
+
+        out_view = out.rearrange("(a p) s -> p a s", p=P)
+        hidden = {}
+
+        def first_layer(e):
+            lists = offsets[:, e * C // 16 : (e + 1) * C // 16]
+            if e >= HOT:
+                f = e - HOT
+                raw = w1c_first[:, f, :] if f < 2 else w1c_rest[:, f - 2, :]
+                w1p = work.tile([P, 2 * H], U8, name="w1p_cold", align_bytes=64)
+                nc.vector.tensor_copy(
+                    w1p[:].bitcast(U16).rearrange("p (t m) -> p t m", t=PACK),
+                    raw.bitcast(U16).rearrange("p (m t) -> p t m", t=PACK),
+                )
+                s1p = work.tile([P, H], U8, name="s1p_cold", align_bytes=64)
+                nc.vector.tensor_copy(
+                    s1p[:].rearrange("p (t m) -> p t m", t=PACK),
+                    s1c[:, f, :].rearrange("p (m t) -> p t m", t=PACK),
+                )
+                lhs = [w1p[:, 2 * P * t : 2 * P * (t + 1)].bitcast(FP4X4) for t in range(PACK)]
+                lhs_s = [s1p[:, P * t : P * (t + 1)] for t in range(PACK)]
+            else:
+                w1p = work.tile([P, H], I32, name="w1p_hot", align_bytes=64)
+                nc.vector.tensor_copy(
+                    w1p[:].rearrange("p (t g i) -> p g t i", t=PACK, i=4),
+                    w1h[:, e, :].rearrange("p (g i t) -> p g t i", t=PACK, i=4),
+                )
+                if e == 0:
+                    nc.vector.tensor_copy(
+                        s1h_perm[:].rearrange("p (t m) -> p t m", t=PACK),
+                        s1h[:].rearrange("p (m t) -> p t m", t=PACK),
+                    )
+                lhs = [w1p[:, P * t : P * (t + 1)].bitcast(FP8X4) for t in range(PACK)]
+                lhs_s = [s1h_perm[4 * e : P, P * t : P * (t + 1)] for t in range(PACK)]
+            gw = work.tile([P, C], U32, name="gw", align_bytes=64)
+            nc.vector.tensor_copy(gw[:], xw[:].indirect(lists))
+            gs = work.tile([P, C], U8, name="gs", align_bytes=64)
+            nc.vector.tensor_copy(gs[:], xs[:].indirect(lists))
+            h = work.tile([P, C, PACK], BF16, name="h", align_bytes=64)
+            for u in range(C // HALF):
+                cols = slice(u * HALF, (u + 1) * HALF)
+                bank = psum1.tile([P, PACK, HALF], F32, name="bank1")
+                for t in range(PACK):
+                    nc.tensor.matmul_mx(
+                        out=bank[:, t, :], lhsT=lhs[t], lhsT_scale=lhs_s[t],
+                        rhs=gw[:, cols].bitcast(FP8X4), rhs_scale=gs[:, cols], start=True, stop=True,
+                    )
+                nc.scalar.activation(h[:, cols, :], bank[:].rearrange("p t n -> p n t"), GELU)
+            hidden[e] = h
+
+        def second_layer(e):
+            hw = work.tile([P, C], U32, name="hw", align_bytes=64)
+            hs = work.tile([P, C], U8, name="hs", align_bytes=64)
+            nc.vector.quantize_mx(
+                out=hw[:].bitcast(FP8X4), scales=hs[:], in_=hidden[e][:].rearrange("p n t -> p (n t)")
+            )
+            bank = psum2.tile([P, N // P, C], F32, name="bank2")
+            for a in range(N // P):
+                if e >= HOT:
+                    lhs = w2c[:, e - HOT, 2 * P * a : 2 * P * (a + 1)].bitcast(FP4X4)
+                    lhs_s = s2c[:, e - HOT, P * a : P * (a + 1)]
+                else:
+                    lhs = w2h[:, e, P * a : P * (a + 1)].bitcast(FP8X4)
+                    lhs_s = s2h[4 * e : P, P * a : P * (a + 1)]
+                nc.tensor.matmul_mx(
+                    out=bank[:, a, :], lhsT=lhs, lhsT_scale=lhs_s,
+                    rhs=hw[:].bitcast(FP8X4), rhs_scale=hs[:], start=True, stop=True,
+                )
+            y = work.tile([P, N // P, C], F32, name="y")
+            nc.scalar.copy(y[:], bank[:])
+            nc.sync.dma_start(out_view[:, :, e * C : (e + 1) * C], y[:])
+
+        for step in range(E + LAG):
+            if step < E:
+                first_layer(ORDER[step])
+            if step >= LAG:
+                second_layer(ORDER[step - LAG])

@@ -1,6 +1,7 @@
 from contextlib import ExitStack
 
 import concourse.mybir as mybir
+from concourse.masks import make_identity
 
 K, T, E, C, H, N, HOT = 512, 1280, 10, 256, 512, 256, 2
 COLD = E - HOT
@@ -20,7 +21,10 @@ P = 128
 PACK = 4
 HALF = 128
 ORDER = [2, 3, 4, 5, 6, 7, 8, 9, 0, 1]
-LAG = 2
+UNITS = [(e, [0, 1]) for e in ORDER[:-1]] + [(ORDER[-1], [0]), (ORDER[-1], [1])]
+TURNS_ON_SCALAR = 2
+OUTS_ON_VECTOR = 1
+FIRST = 3
 
 
 def tile_moe_hot_s_mlp_gelu_kernel(
@@ -30,126 +34,138 @@ def tile_moe_hot_s_mlp_gelu_kernel(
     nc = tc.nc
     with ExitStack() as ctx:
         held = ctx.enter_context(tc.tile_pool(name="held", bufs=1))
-        work = ctx.enter_context(tc.tile_pool(name="work", bufs=4))
-        psum1 = ctx.enter_context(tc.psum_pool(name="psum1", bufs=6))
+        work = ctx.enter_context(tc.tile_pool(name="work", bufs=6))
+        feed = ctx.enter_context(tc.tile_pool(name="feed", bufs=4))
+        psum1 = ctx.enter_context(tc.psum_pool(name="psum1", bufs=4))
+        psumt = ctx.enter_context(tc.psum_pool(name="psumt", bufs=2))
         psum2 = ctx.enter_context(tc.psum_pool(name="psum2", bufs=2))
 
         offsets = held.tile([P, E * C // 16], U16, name="offsets")
         xw = held.tile([P, T], U32, name="xw", align_bytes=64)
         xs = held.tile([P, T], U8, name="xs", align_bytes=64)
-        w1c_first = held.tile([P, 2, 2 * H], U8, name="w1c_first", align_bytes=64)
-        w1c_rest = held.tile([P, COLD - 2, 2 * H], U8, name="w1c_rest", align_bytes=64)
-        w1h = held.tile([P, HOT, H], I32, name="w1h", align_bytes=64)
-        w2c = held.tile([P, COLD, 2 * N], U8, name="w2c", align_bytes=64)
-        w2h = held.tile([P, HOT, N], I32, name="w2h", align_bytes=64)
-        s1c = held.tile([P, COLD, H], U8, name="s1c", align_bytes=64)
-        s2c = held.tile([P, COLD, N], U8, name="s2c", align_bytes=64)
-        s1h = held.tile([P, H], U8, name="s1h", align_bytes=64)
-        s2h = held.tile([P, N], U8, name="s2h", align_bytes=64)
-        s1h_perm = held.tile([P, H], U8, name="s1h_perm", align_bytes=64)
+        ident = held.tile([P, P], F32, name="ident")
         warm = held.tile([P, 16], F32, name="warm")
         warm_out = held.tile([P, 16], BF16, name="warm_out")
+        w1c_first = held.tile([P, FIRST, 2 * H], U8, name="w1c_first", align_bytes=64)
+        w1c_rest = held.tile([P, COLD - FIRST, 2 * H], U8, name="w1c_rest", align_bytes=64)
+        s1c_first = held.tile([P, FIRST, H], U8, name="s1c_first", align_bytes=64)
+        s1c_rest = held.tile([P, COLD - FIRST, H], U8, name="s1c_rest", align_bytes=64)
+        w2c = held.tile([P, COLD, 2 * N], U8, name="w2c", align_bytes=64)
+        s2c = held.tile([P, COLD, N], U8, name="s2c", align_bytes=64)
+        w1h = held.tile([P, HOT, H], I32, name="w1h", align_bytes=64)
+        w2h = held.tile([P, HOT, N], I32, name="w2h", align_bytes=64)
+        s1h = held.tile([P, H], U8, name="s1h", align_bytes=64)
+        s2h = held.tile([P, N], U8, name="s2h", align_bytes=64)
 
-        nc.vector.memset(s1c[:].rearrange("p e n -> p (e n)").bitcast(I32), 0)
         nc.gpsimd.memset(xs[:].bitcast(I32), 0)
+        make_identity(nc, ident[:])
+        nc.vector.memset(s1c_first[:].rearrange("p e n -> p (e n)").bitcast(I32), 0)
+        nc.vector.memset(warm[:], 0.0)
         nc.vector.memset(s2c[:].rearrange("p e n -> p (e n)").bitcast(I32), 0)
+        nc.vector.memset(s1c_rest[:].rearrange("p e n -> p (e n)").bitcast(I32), 0)
         nc.vector.memset(s1h[:].bitcast(I32), 0)
         nc.vector.memset(s2h[:].bitcast(I32), 0)
-        nc.gpsimd.memset(warm[:], 0.0)
-        nc.scalar.activation(warm_out[:], warm[:], GELU)
 
-        def load_cold_words(tile, words):
-            nc.sync.dma_start(tile[:].bitcast(I32), words.rearrange("e s p b -> p (e s) b").bitcast(I32))
+        def load_cold_words(queue, tile, words):
+            queue.dma_start(tile.bitcast(I32), words.rearrange("e s p b -> p (e s) b").bitcast(I32))
 
-        def load_hot_words(tile, words):
-            nc.sync.dma_start(tile[:], words.rearrange("e s p n d -> p (e s) (n d)").bitcast(I32))
+        def load_hot_words(queue, tile, words):
+            queue.dma_start(tile.bitcast(I32), words.rearrange("e s p n d -> p (e s) (n d)").bitcast(I32))
 
-        def load_cold_scales(tile, scales):
-            for q in range(4):
-                nc.sync.dma_start(
+        def load_cold_scales(queue, tile, scales, quadrants):
+            for q in quadrants:
+                queue.dma_start(
                     tile[32 * q : 32 * q + 4, :, :].bitcast(I32),
                     scales[:, 0, 4 * q : 4 * q + 4, :].rearrange("e r n -> r e n").bitcast(I32),
                 )
 
-        def load_hot_scales(tile, scales):
+        def load_hot_scales(queue, tile, scales):
             for q in range(4):
-                nc.sync.dma_start(
+                queue.dma_start(
                     tile[32 * q : 32 * q + 4 * HOT, :].bitcast(I32),
                     scales[:, 0, 4 * q : 4 * q + 4, :].bitcast(I32),
                 )
 
+        def load_token_scales(queue, q):
+            queue.dma_start(xs[32 * q : 32 * q + 4, :].bitcast(I32), x_scales[0, 4 * q : 4 * q + 4, :].bitcast(I32))
+
         nc.sync.dma_start(offsets[:], offs)
+        load_token_scales(nc.scalar, 2)
+        load_token_scales(nc.sync, 0)
+        load_token_scales(nc.scalar, 3)
+        load_token_scales(nc.sync, 1)
         nc.sync.dma_start(xw[:].bitcast(I32), x_words[0].rearrange("p t d -> p (t d)").bitcast(I32))
-        load_cold_words(w1c_first, w1c_words[0:2])
-        load_cold_scales(s1c, w1c_scales)
-        for q in range(4):
-            nc.sync.dma_start(
-                xs[32 * q : 32 * q + 4, :].bitcast(I32), x_scales[0, 4 * q : 4 * q + 4, :].bitcast(I32)
-            )
-        load_cold_words(w1c_rest, w1c_words[2:COLD])
-        load_cold_scales(s2c, w2c_scales)
-        load_cold_words(w2c, w2c_words)
-        load_hot_words(w1h, w1h_words)
-        load_hot_scales(s1h, w1h_scales)
-        load_hot_words(w2h, w2h_words)
-        load_hot_scales(s2h, w2h_scales)
+        load_cold_scales(nc.scalar, s1c_first, w1c_scales[0:FIRST], [0, 1])
+        load_cold_scales(nc.sync, s1c_first, w1c_scales[0:FIRST], [2, 3])
+        load_cold_words(nc.sync, w1c_first[:], w1c_words[0:FIRST])
+        nc.scalar.activation(warm_out[:], warm[:], GELU)
+        load_cold_scales(nc.scalar, s2c, w2c_scales, range(4))
+        load_cold_words(nc.sync, w2c[:], w2c_words)
+        load_cold_words(nc.sync, w1c_rest[:], w1c_words[FIRST:COLD])
+        load_cold_scales(nc.sync, s1c_rest, w1c_scales[FIRST:COLD], range(4))
+
+        def load_hot():
+            load_hot_words(nc.sync, w1h[:], w1h_words)
+            load_hot_scales(nc.sync, s1h, w1h_scales)
+            load_hot_words(nc.sync, w2h[:], w2h_words)
+            load_hot_scales(nc.sync, s2h, w2h_scales)
 
         out_view = out.rearrange("(a p) s -> p a s", p=P)
+        by_slot = {}
         hidden = {}
 
         def first_layer(e):
             lists = offsets[:, e * C // 16 : (e + 1) * C // 16]
             if e >= HOT:
                 f = e - HOT
-                raw = w1c_first[:, f, :] if f < 2 else w1c_rest[:, f - 2, :]
-                w1p = work.tile([P, 2 * H], U8, name="w1p_cold", align_bytes=64)
-                nc.vector.tensor_copy(
-                    w1p[:].bitcast(U16).rearrange("p (t m) -> p t m", t=PACK),
-                    raw.bitcast(U16).rearrange("p (m t) -> p t m", t=PACK),
-                )
-                s1p = work.tile([P, H], U8, name="s1p_cold", align_bytes=64)
-                nc.vector.tensor_copy(
-                    s1p[:].rearrange("p (t m) -> p t m", t=PACK),
-                    s1c[:, f, :].rearrange("p (m t) -> p t m", t=PACK),
-                )
-                lhs = [w1p[:, 2 * P * t : 2 * P * (t + 1)].bitcast(FP4X4) for t in range(PACK)]
-                lhs_s = [s1p[:, P * t : P * (t + 1)] for t in range(PACK)]
+                w1 = (w1c_first[:, f, :] if f < FIRST else w1c_rest[:, f - FIRST, :]).bitcast(FP4X4)
+                s1 = s1c_first[:, f, :] if f < FIRST else s1c_rest[:, f - FIRST, :]
             else:
-                w1p = work.tile([P, H], I32, name="w1p_hot", align_bytes=64)
-                nc.vector.tensor_copy(
-                    w1p[:].rearrange("p (t g i) -> p g t i", t=PACK, i=4),
-                    w1h[:, e, :].rearrange("p (g i t) -> p g t i", t=PACK, i=4),
-                )
-                if e == 0:
-                    nc.vector.tensor_copy(
-                        s1h_perm[:].rearrange("p (t m) -> p t m", t=PACK),
-                        s1h[:].rearrange("p (m t) -> p t m", t=PACK),
-                    )
-                lhs = [w1p[:, P * t : P * (t + 1)].bitcast(FP8X4) for t in range(PACK)]
-                lhs_s = [s1h_perm[4 * e : P, P * t : P * (t + 1)] for t in range(PACK)]
-            gw = work.tile([P, C], U32, name="gw", align_bytes=64)
-            nc.vector.tensor_copy(gw[:], xw[:].indirect(lists))
-            gs = work.tile([P, C], U8, name="gs", align_bytes=64)
+                w1 = w1h[:, e, :].bitcast(FP8X4)
+                s1 = s1h[4 * e : P, :]
+            gs = feed.tile([P, C], U8, name="gs", bufs=3, align_bytes=64)
             nc.vector.tensor_copy(gs[:], xs[:].indirect(lists))
-            h = work.tile([P, C, PACK], BF16, name="h", align_bytes=64)
-            for u in range(C // HALF):
-                cols = slice(u * HALF, (u + 1) * HALF)
-                bank = psum1.tile([P, PACK, HALF], F32, name="bank1")
-                for t in range(PACK):
-                    nc.tensor.matmul_mx(
-                        out=bank[:, t, :], lhsT=lhs[t], lhsT_scale=lhs_s[t],
-                        rhs=gw[:, cols].bitcast(FP8X4), rhs_scale=gs[:, cols], start=True, stop=True,
-                    )
-                nc.scalar.activation(h[:, cols, :], bank[:].rearrange("p t n -> p n t"), GELU)
-            hidden[e] = h
+            gw = feed.tile([P, C], U32, name="gw", align_bytes=64)
+            nc.vector.tensor_copy(gw[:], xw[:].indirect(lists))
+            by_slot[e] = []
+            for half in range(C // HALF):
+                cols = slice(half * HALF, (half + 1) * HALF)
+                bank = psum1.tile([P, H], F32, name="bank1")
+                nc.tensor.matmul_mx(
+                    out=bank[:], lhsT=gw[:, cols].bitcast(FP8X4), lhsT_scale=gs[:, cols],
+                    rhs=w1, rhs_scale=s1, start=True, stop=True,
+                )
+                hb = work.tile([P, H], BF16, name="hb", bufs=4, align_bytes=64)
+                nc.scalar.activation(
+                    hb[:].rearrange("s (u p c) -> s u p c", u=2, c=2),
+                    bank[:].rearrange("s (p u c) -> s u p c", u=2, c=2),
+                    GELU,
+                )
+                by_slot[e].append(hb)
 
-        def second_layer(e):
-            hw = work.tile([P, C], U32, name="hw", align_bytes=64)
-            hs = work.tile([P, C], U8, name="hs", align_bytes=64)
-            nc.vector.quantize_mx(
-                out=hw[:].bitcast(FP8X4), scales=hs[:], in_=hidden[e][:].rearrange("p n t -> p (n t)")
-            )
-            bank = psum2.tile([P, N // P, C], F32, name="bank2")
+        def turn(unit):
+            e, halves = UNITS[unit]
+            bank = psumt.tile([P, len(halves), 2, HALF], F32, name="bankt")
+            for j, half in enumerate(halves):
+                words = by_slot[e][half][:].bitcast(F32)
+                for u in range(2):
+                    nc.tensor.transpose(bank[:, j, u, :], words[:, u * P : (u + 1) * P], ident[:])
+            h = work.tile([P, len(halves) * HALF * PACK], BF16, name="h", bufs=2, align_bytes=64)
+            h_words = h[:].bitcast(F32).rearrange("p (j s u) -> p j s u", s=HALF, u=2)
+            turned = bank[:].rearrange("p j u s -> p j s u")
+            if unit < TURNS_ON_SCALAR:
+                nc.scalar.copy(h_words, turned)
+            else:
+                nc.vector.tensor_copy(h_words, turned)
+            hidden[unit] = h
+
+        def second_layer(unit):
+            e, halves = UNITS[unit]
+            width = len(halves) * HALF
+            hw = work.tile([P, width], U32, name="hw", bufs=2, align_bytes=64)
+            hs = work.tile([P, width], U8, name="hs", bufs=2, align_bytes=64)
+            nc.vector.quantize_mx(out=hw[:].bitcast(FP8X4), scales=hs[:], in_=hidden[unit][:])
+            bank = psum2.tile([P, N // P, width], F32, name="bank2")
             for a in range(N // P):
                 if e >= HOT:
                     lhs = w2c[:, e - HOT, 2 * P * a : 2 * P * (a + 1)].bitcast(FP4X4)
@@ -161,12 +177,20 @@ def tile_moe_hot_s_mlp_gelu_kernel(
                     out=bank[:, a, :], lhsT=lhs, lhsT_scale=lhs_s,
                     rhs=hw[:].bitcast(FP8X4), rhs_scale=hs[:], start=True, stop=True,
                 )
-            y = work.tile([P, N // P, C], F32, name="y")
-            nc.scalar.copy(y[:], bank[:])
-            nc.sync.dma_start(out_view[:, :, e * C : (e + 1) * C], y[:])
+            y = work.tile([P, N // P, width], F32, name="y")
+            if unit >= len(UNITS) - OUTS_ON_VECTOR:
+                nc.vector.tensor_copy(y[:], bank[:])
+            else:
+                nc.scalar.copy(y[:], bank[:])
+            first = e * C + halves[0] * HALF
+            nc.sync.dma_start(out_view[:, :, first : first + width], y[:])
 
-        for step in range(E + LAG):
+        for step in range(len(UNITS) + 2):
             if step < E:
                 first_layer(ORDER[step])
-            if step >= LAG:
-                second_layer(ORDER[step - LAG])
+            if 1 <= step <= len(UNITS):
+                turn(step - 1)
+            if step >= 2:
+                second_layer(step - 2)
+            if step == 3:
+                load_hot()

@@ -20,11 +20,11 @@ GELU = mybir.ActivationFunctionType.Gelu_apprx_tanh
 P = 128
 PACK = 4
 HALF = 128
-ORDER = [2, 3, 4, 5, 6, 7, 8, 9, 0, 1]
+ORDER = [2, 3, 4, 5, 6, 7, 0, 8, 1, 9]
+TURNED = [2, 4, 6, 0, 1]
 UNITS = [(e, [0, 1]) for e in ORDER[:-1]] + [(ORDER[-1], [0]), (ORDER[-1], [1])]
-TURNS_ON_SCALAR = 2
-OUTS_ON_VECTOR = 1
-FIRST = 3
+FIRST = 2
+OUTS_ON_VECTOR = [4, 5, 9, 10]
 
 
 def tile_moe_hot_s_mlp_gelu_kernel(
@@ -37,8 +37,8 @@ def tile_moe_hot_s_mlp_gelu_kernel(
         work = ctx.enter_context(tc.tile_pool(name="work", bufs=6))
         feed = ctx.enter_context(tc.tile_pool(name="feed", bufs=4))
         psum1 = ctx.enter_context(tc.psum_pool(name="psum1", bufs=4))
-        psumt = ctx.enter_context(tc.psum_pool(name="psumt", bufs=2))
-        psum2 = ctx.enter_context(tc.psum_pool(name="psum2", bufs=2))
+        psumt = ctx.enter_context(tc.psum_pool(name="psumt", bufs=1))
+        psum2 = ctx.enter_context(tc.psum_pool(name="psum2", bufs=3))
 
         offsets = held.tile([P, E * C // 16], U16, name="offsets")
         xw = held.tile([P, T], U32, name="xw", align_bytes=64)
@@ -61,8 +61,8 @@ def tile_moe_hot_s_mlp_gelu_kernel(
         make_identity(nc, ident[:])
         nc.vector.memset(s1c_first[:].rearrange("p e n -> p (e n)").bitcast(I32), 0)
         nc.vector.memset(warm[:], 0.0)
-        nc.vector.memset(s2c[:].rearrange("p e n -> p (e n)").bitcast(I32), 0)
         nc.vector.memset(s1c_rest[:].rearrange("p e n -> p (e n)").bitcast(I32), 0)
+        nc.vector.memset(s2c[:].rearrange("p e n -> p (e n)").bitcast(I32), 0)
         nc.vector.memset(s1h[:].bitcast(I32), 0)
         nc.vector.memset(s2h[:].bitcast(I32), 0)
 
@@ -90,25 +90,22 @@ def tile_moe_hot_s_mlp_gelu_kernel(
             queue.dma_start(xs[32 * q : 32 * q + 4, :].bitcast(I32), x_scales[0, 4 * q : 4 * q + 4, :].bitcast(I32))
 
         nc.sync.dma_start(offsets[:], offs)
-        load_token_scales(nc.scalar, 2)
-        load_token_scales(nc.sync, 0)
-        load_token_scales(nc.scalar, 3)
-        load_token_scales(nc.sync, 1)
+        load_token_scales(nc.scalar, 0)
+        load_token_scales(nc.scalar, 1)
+        nc.scalar.activation(warm_out[:], warm[:], GELU)
+        load_token_scales(nc.sync, 2)
+        load_token_scales(nc.sync, 3)
         nc.sync.dma_start(xw[:].bitcast(I32), x_words[0].rearrange("p t d -> p (t d)").bitcast(I32))
         load_cold_scales(nc.scalar, s1c_first, w1c_scales[0:FIRST], [0, 1])
-        load_cold_scales(nc.sync, s1c_first, w1c_scales[0:FIRST], [2, 3])
         load_cold_words(nc.sync, w1c_first[:], w1c_words[0:FIRST])
-        nc.scalar.activation(warm_out[:], warm[:], GELU)
-        load_cold_scales(nc.scalar, s2c, w2c_scales, range(4))
-        load_cold_words(nc.sync, w2c[:], w2c_words)
+        load_cold_scales(nc.scalar, s1c_first, w1c_scales[0:FIRST], [2])
+        load_cold_scales(nc.sync, s1c_first, w1c_scales[0:FIRST], [3])
+        load_cold_scales(nc.sync, s1c_rest, w1c_scales[FIRST:COLD], [0, 1])
         load_cold_words(nc.sync, w1c_rest[:], w1c_words[FIRST:COLD])
-        load_cold_scales(nc.sync, s1c_rest, w1c_scales[FIRST:COLD], range(4))
-
-        def load_hot():
-            load_hot_words(nc.sync, w1h[:], w1h_words)
-            load_hot_scales(nc.sync, s1h, w1h_scales)
-            load_hot_words(nc.sync, w2h[:], w2h_words)
-            load_hot_scales(nc.sync, s2h, w2h_scales)
+        load_cold_scales(nc.scalar, s1c_rest, w1c_scales[FIRST:COLD], [2, 3])
+        load_cold_words(nc.sync, w2c[:], w2c_words)
+        load_cold_scales(nc.scalar, s2c, w2c_scales, [0, 1])
+        load_cold_scales(nc.sync, s2c, w2c_scales, [2, 3])
 
         out_view = out.rearrange("(a p) s -> p a s", p=P)
         by_slot = {}
@@ -118,53 +115,78 @@ def tile_moe_hot_s_mlp_gelu_kernel(
             lists = offsets[:, e * C // 16 : (e + 1) * C // 16]
             if e >= HOT:
                 f = e - HOT
-                w1 = (w1c_first[:, f, :] if f < FIRST else w1c_rest[:, f - FIRST, :]).bitcast(FP4X4)
+                w1 = w1c_first[:, f, :] if f < FIRST else w1c_rest[:, f - FIRST, :]
                 s1 = s1c_first[:, f, :] if f < FIRST else s1c_rest[:, f - FIRST, :]
+                fmt = FP4X4
             else:
-                w1 = w1h[:, e, :].bitcast(FP8X4)
+                w1 = w1h[:, e, :]
                 s1 = s1h[4 * e : P, :]
+                fmt = FP8X4
+            if e not in TURNED:
+                w1p = feed.tile([P, 2 * H], U8, name="w1p", bufs=2, align_bytes=64)
+                nc.vector.tensor_copy(
+                    w1p[:].bitcast(U16).rearrange("p (t m) -> p t m", t=PACK),
+                    w1.bitcast(U16).rearrange("p (m t) -> p t m", t=PACK),
+                )
+                s1p = feed.tile([P, H], U8, name="s1p", bufs=2, align_bytes=64)
+                nc.vector.tensor_copy(
+                    s1p[:].rearrange("p (t m) -> p t m", t=PACK), s1.rearrange("p (m t) -> p t m", t=PACK)
+                )
             gs = feed.tile([P, C], U8, name="gs", bufs=3, align_bytes=64)
             nc.vector.tensor_copy(gs[:], xs[:].indirect(lists))
-            gw = feed.tile([P, C], U32, name="gw", align_bytes=64)
+            gw = feed.tile([P, C], U32, name="gw", bufs=2, align_bytes=64)
             nc.vector.tensor_copy(gw[:], xw[:].indirect(lists))
+            if e not in TURNED:
+                hidden[e] = work.tile([P, C * PACK], BF16, name="h", bufs=2, align_bytes=64)
             by_slot[e] = []
             for half in range(C // HALF):
                 cols = slice(half * HALF, (half + 1) * HALF)
                 bank = psum1.tile([P, H], F32, name="bank1")
-                nc.tensor.matmul_mx(
-                    out=bank[:], lhsT=gw[:, cols].bitcast(FP8X4), lhsT_scale=gs[:, cols],
-                    rhs=w1, rhs_scale=s1, start=True, stop=True,
-                )
-                hb = work.tile([P, H], BF16, name="hb", bufs=4, align_bytes=64)
-                nc.scalar.activation(
-                    hb[:].rearrange("s (u p c) -> s u p c", u=2, c=2),
-                    bank[:].rearrange("s (p u c) -> s u p c", u=2, c=2),
-                    GELU,
-                )
-                by_slot[e].append(hb)
+                if e in TURNED:
+                    nc.tensor.matmul_mx(
+                        out=bank[:], lhsT=gw[:, cols].bitcast(FP8X4), lhsT_scale=gs[:, cols],
+                        rhs=w1.bitcast(fmt), rhs_scale=s1, start=True, stop=True,
+                    )
+                    hb = work.tile([P, H], BF16, name="hb", bufs=2, align_bytes=64)
+                    nc.scalar.activation(
+                        hb[:].rearrange("s (u p c) -> s u p c", u=2, c=2),
+                        bank[:].rearrange("s (p u c) -> s u p c", u=2, c=2),
+                        GELU,
+                    )
+                    by_slot[e].append(hb)
+                else:
+                    for t in range(PACK):
+                        nc.tensor.matmul_mx(
+                            out=bank[:, t * HALF : (t + 1) * HALF],
+                            lhsT=w1p[:, 2 * P * t : 2 * P * (t + 1)].bitcast(fmt),
+                            lhsT_scale=s1p[:, P * t : P * (t + 1)],
+                            rhs=gw[:, cols].bitcast(FP8X4), rhs_scale=gs[:, cols], start=True, stop=True,
+                        )
+                    nc.scalar.activation(
+                        hidden[e][:, half * H : (half + 1) * H].rearrange("p (s t) -> p s t", t=PACK),
+                        bank[:].rearrange("p (t s) -> p s t", t=PACK),
+                        GELU,
+                    )
 
-        def turn(unit):
-            e, halves = UNITS[unit]
-            bank = psumt.tile([P, len(halves), 2, HALF], F32, name="bankt")
-            for j, half in enumerate(halves):
+        def turn(e):
+            bank = psumt.tile([P, C // HALF, 2, HALF], F32, name="bankt")
+            for half in range(C // HALF):
                 words = by_slot[e][half][:].bitcast(F32)
                 for u in range(2):
-                    nc.tensor.transpose(bank[:, j, u, :], words[:, u * P : (u + 1) * P], ident[:])
-            h = work.tile([P, len(halves) * HALF * PACK], BF16, name="h", bufs=2, align_bytes=64)
-            h_words = h[:].bitcast(F32).rearrange("p (j s u) -> p j s u", s=HALF, u=2)
-            turned = bank[:].rearrange("p j u s -> p j s u")
-            if unit < TURNS_ON_SCALAR:
-                nc.scalar.copy(h_words, turned)
+                    nc.tensor.transpose(bank[:, half, u, :], words[:, u * P : (u + 1) * P], ident[:])
+            hidden[e] = work.tile([P, C * PACK], BF16, name="h", bufs=2, align_bytes=64)
+            h_words = hidden[e][:].bitcast(F32).rearrange("p (j s u) -> p j s u", s=HALF, u=2)
+            if e < HOT:
+                nc.vector.tensor_copy(h_words, bank[:].rearrange("p j u s -> p j s u"))
             else:
-                nc.vector.tensor_copy(h_words, turned)
-            hidden[unit] = h
+                nc.scalar.copy(h_words, bank[:].rearrange("p j u s -> p j s u"))
 
         def second_layer(unit):
             e, halves = UNITS[unit]
             width = len(halves) * HALF
-            hw = work.tile([P, width], U32, name="hw", bufs=2, align_bytes=64)
-            hs = work.tile([P, width], U8, name="hs", bufs=2, align_bytes=64)
-            nc.vector.quantize_mx(out=hw[:].bitcast(FP8X4), scales=hs[:], in_=hidden[unit][:])
+            hw = work.tile([P, width], U32, name="hw", bufs=5, align_bytes=64)
+            hs = work.tile([P, width], U8, name="hs", bufs=5, align_bytes=64)
+            nc.vector.quantize_mx(out=hw[:].bitcast(FP8X4), scales=hs[:], in_=hidden[e][:, halves[0] * H : (halves[-1] + 1) * H])
             bank = psum2.tile([P, N // P, width], F32, name="bank2")
             for a in range(N // P):
                 if e >= HOT:
@@ -178,7 +200,7 @@ def tile_moe_hot_s_mlp_gelu_kernel(
                     rhs=hw[:].bitcast(FP8X4), rhs_scale=hs[:], start=True, stop=True,
                 )
             y = work.tile([P, N // P, width], F32, name="y")
-            if unit >= len(UNITS) - OUTS_ON_VECTOR:
+            if unit in OUTS_ON_VECTOR:
                 nc.vector.tensor_copy(y[:], bank[:])
             else:
                 nc.scalar.copy(y[:], bank[:])
@@ -188,9 +210,12 @@ def tile_moe_hot_s_mlp_gelu_kernel(
         for step in range(len(UNITS) + 2):
             if step < E:
                 first_layer(ORDER[step])
-            if 1 <= step <= len(UNITS):
-                turn(step - 1)
+            if 1 <= step <= E and ORDER[step - 1] in TURNED:
+                turn(ORDER[step - 1])
             if step >= 2:
                 second_layer(step - 2)
-            if step == 3:
-                load_hot()
+            if step == 1:
+                load_hot_words(nc.sync, w1h[:], w1h_words)
+                load_hot_scales(nc.sync, s1h, w1h_scales)
+                load_hot_words(nc.sync, w2h[:], w2h_words)
+                load_hot_scales(nc.sync, s2h, w2h_scales)

@@ -20,11 +20,10 @@ GELU = mybir.ActivationFunctionType.Gelu_apprx_tanh
 P = 128
 PACK = 4
 HALF = 128
-ORDER = [2, 3, 4, 5, 6, 7, 0, 8, 1, 9]
-TURNED = [2, 4, 6, 0, 1]
-UNITS = [(e, [0, 1]) for e in ORDER[:-1]] + [(ORDER[-1], [0]), (ORDER[-1], [1])]
-FIRST = 2
-OUTS_ON_VECTOR = [4, 5, 9, 10]
+UNITS = [(e, [0, 1]) for e in range(E - 1)] + [(E - 1, [0]), (E - 1, [1])]
+OUTS_ON_VECTOR = [6, 8, 10]
+LAG = 2
+FIRST = 3
 
 
 def tile_moe_hot_s_mlp_gelu_kernel(
@@ -34,11 +33,10 @@ def tile_moe_hot_s_mlp_gelu_kernel(
     nc = tc.nc
     with ExitStack() as ctx:
         held = ctx.enter_context(tc.tile_pool(name="held", bufs=1))
-        work = ctx.enter_context(tc.tile_pool(name="work", bufs=6))
-        feed = ctx.enter_context(tc.tile_pool(name="feed", bufs=4))
+        work = ctx.enter_context(tc.tile_pool(name="work", bufs=4))
+        feed = ctx.enter_context(tc.tile_pool(name="feed", bufs=3))
         psum1 = ctx.enter_context(tc.psum_pool(name="psum1", bufs=4))
-        psumt = ctx.enter_context(tc.psum_pool(name="psumt", bufs=1))
-        psum2 = ctx.enter_context(tc.psum_pool(name="psum2", bufs=3))
+        psum2 = ctx.enter_context(tc.psum_pool(name="psum2", bufs=4))
 
         offsets = held.tile([P, E * C // 16], U16, name="offsets")
         xw = held.tile([P, T], U32, name="xw", align_bytes=64)
@@ -48,29 +46,26 @@ def tile_moe_hot_s_mlp_gelu_kernel(
         warm_out = held.tile([P, 16], BF16, name="warm_out")
         w1c_first = held.tile([P, FIRST, 2 * H], U8, name="w1c_first", align_bytes=64)
         w1c_rest = held.tile([P, COLD - FIRST, 2 * H], U8, name="w1c_rest", align_bytes=64)
-        s1c_first = held.tile([P, FIRST, H], U8, name="s1c_first", align_bytes=64)
-        s1c_rest = held.tile([P, COLD - FIRST, H], U8, name="s1c_rest", align_bytes=64)
+        s1c_rows = held.tile([P, H], U8, name="s1c_rows", align_bytes=64)
+        s1c_moved = held.tile([P, H], U8, name="s1c_moved", align_bytes=64)
+        s1c = held.tile([P, COLD, H], U8, name="s1c", align_bytes=64)
         w2c = held.tile([P, COLD, 2 * N], U8, name="w2c", align_bytes=64)
         s2c = held.tile([P, COLD, N], U8, name="s2c", align_bytes=64)
-        w1h = held.tile([P, HOT, H], I32, name="w1h", align_bytes=64)
+        w1h = [held.tile([P, H], I32, name="w1h%d" % e, align_bytes=64) for e in range(HOT)]
         w2h = held.tile([P, HOT, N], I32, name="w2h", align_bytes=64)
         s1h = held.tile([P, H], U8, name="s1h", align_bytes=64)
         s2h = held.tile([P, N], U8, name="s2h", align_bytes=64)
 
         nc.gpsimd.memset(xs[:].bitcast(I32), 0)
         make_identity(nc, ident[:])
-        nc.vector.memset(s1c_first[:].rearrange("p e n -> p (e n)").bitcast(I32), 0)
-        nc.vector.memset(warm[:], 0.0)
-        nc.vector.memset(s1c_rest[:].rearrange("p e n -> p (e n)").bitcast(I32), 0)
-        nc.vector.memset(s2c[:].rearrange("p e n -> p (e n)").bitcast(I32), 0)
         nc.vector.memset(s1h[:].bitcast(I32), 0)
+        nc.vector.memset(warm[:], 0.0)
+        nc.vector.memset(s1c[:].rearrange("p e n -> p (e n)").bitcast(I32), 0)
         nc.vector.memset(s2h[:].bitcast(I32), 0)
+        nc.vector.memset(s2c[:].rearrange("p e n -> p (e n)").bitcast(I32), 0)
 
         def load_cold_words(queue, tile, words):
             queue.dma_start(tile.bitcast(I32), words.rearrange("e s p b -> p (e s) b").bitcast(I32))
-
-        def load_hot_words(queue, tile, words):
-            queue.dma_start(tile.bitcast(I32), words.rearrange("e s p n d -> p (e s) (n d)").bitcast(I32))
 
         def load_cold_scales(queue, tile, scales, quadrants):
             for q in quadrants:
@@ -79,8 +74,8 @@ def tile_moe_hot_s_mlp_gelu_kernel(
                     scales[:, 0, 4 * q : 4 * q + 4, :].rearrange("e r n -> r e n").bitcast(I32),
                 )
 
-        def load_hot_scales(queue, tile, scales):
-            for q in range(4):
+        def load_hot_scales(queue, tile, scales, quadrants):
+            for q in quadrants:
                 queue.dma_start(
                     tile[32 * q : 32 * q + 4 * HOT, :].bitcast(I32),
                     scales[:, 0, 4 * q : 4 * q + 4, :].bitcast(I32),
@@ -90,22 +85,29 @@ def tile_moe_hot_s_mlp_gelu_kernel(
             queue.dma_start(xs[32 * q : 32 * q + 4, :].bitcast(I32), x_scales[0, 4 * q : 4 * q + 4, :].bitcast(I32))
 
         nc.sync.dma_start(offsets[:], offs)
+        nc.scalar.dma_start(s1c_rows[:].bitcast(I32), w1c_scales.rearrange("f s b n -> (s b) f n").bitcast(I32))
         load_token_scales(nc.scalar, 0)
         load_token_scales(nc.scalar, 1)
-        nc.scalar.activation(warm_out[:], warm[:], GELU)
         load_token_scales(nc.sync, 2)
         load_token_scales(nc.sync, 3)
         nc.sync.dma_start(xw[:].bitcast(I32), x_words[0].rearrange("p t d -> p (t d)").bitcast(I32))
-        load_cold_scales(nc.scalar, s1c_first, w1c_scales[0:FIRST], [0, 1])
+        load_hot_scales(nc.scalar, s1h, w1h_scales, range(4))
+        nc.scalar.activation(warm_out[:], warm[:], GELU)
+        nc.sync.dma_start(w1h[0][:], w1h_words[0, 0].rearrange("p n d -> p (n d)").bitcast(I32))
+        nc.sync.dma_start(w1h[1][:], w1h_words[1, 0].rearrange("p n d -> p (n d)").bitcast(I32))
         load_cold_words(nc.sync, w1c_first[:], w1c_words[0:FIRST])
-        load_cold_scales(nc.scalar, s1c_first, w1c_scales[0:FIRST], [2])
-        load_cold_scales(nc.sync, s1c_first, w1c_scales[0:FIRST], [3])
-        load_cold_scales(nc.sync, s1c_rest, w1c_scales[FIRST:COLD], [0, 1])
+        nc.vector.tensor_copy(
+            s1c_moved[:].rearrange("p (t m) -> p t m", t=PACK), s1c_rows[:].rearrange("p (m t) -> p t m", t=PACK)
+        )
+        for q in range(4):
+            nc.sync.dma_start(
+                s1c[32 * q : 32 * q + 4, :, :].bitcast(I32), s1c_moved[32 * q : 32 * q + 32, :].bitcast(I32)
+            )
+        nc.sync.dma_start(w2h[:], w2h_words.rearrange("e s p n d -> p (e s) (n d)").bitcast(I32))
+        load_hot_scales(nc.sync, s2h, w2h_scales, range(4))
         load_cold_words(nc.sync, w1c_rest[:], w1c_words[FIRST:COLD])
-        load_cold_scales(nc.scalar, s1c_rest, w1c_scales[FIRST:COLD], [2, 3])
         load_cold_words(nc.sync, w2c[:], w2c_words)
-        load_cold_scales(nc.scalar, s2c, w2c_scales, [0, 1])
-        load_cold_scales(nc.sync, s2c, w2c_scales, [2, 3])
+        load_cold_scales(nc.sync, s2c, w2c_scales, range(4))
 
         out_view = out.rearrange("(a p) s -> p a s", p=P)
         by_slot = {}
@@ -113,41 +115,29 @@ def tile_moe_hot_s_mlp_gelu_kernel(
 
         def first_layer(e):
             lists = offsets[:, e * C // 16 : (e + 1) * C // 16]
+            gs = feed.tile([P, C], U8, name="gs", bufs=2, align_bytes=64)
+            nc.vector.tensor_copy(gs[:], xs[:].indirect(lists))
+            gw = feed.tile([P, C], U32, name="gw", align_bytes=64)
+            nc.vector.tensor_copy(gw[:], xw[:].indirect(lists))
             if e >= HOT:
                 f = e - HOT
                 w1 = w1c_first[:, f, :] if f < FIRST else w1c_rest[:, f - FIRST, :]
-                s1 = s1c_first[:, f, :] if f < FIRST else s1c_rest[:, f - FIRST, :]
-                fmt = FP4X4
-            else:
-                w1 = w1h[:, e, :]
-                s1 = s1h[4 * e : P, :]
-                fmt = FP8X4
-            if e not in TURNED:
-                w1p = feed.tile([P, 2 * H], U8, name="w1p", bufs=2, align_bytes=64)
-                nc.vector.tensor_copy(
+                w1p = feed.tile([P, 2 * H], U8, name="w1p", bufs=8, align_bytes=64)
+                nc.gpsimd.tensor_copy(
                     w1p[:].bitcast(U16).rearrange("p (t m) -> p t m", t=PACK),
                     w1.bitcast(U16).rearrange("p (m t) -> p t m", t=PACK),
                 )
-                s1p = feed.tile([P, H], U8, name="s1p", bufs=2, align_bytes=64)
-                nc.vector.tensor_copy(
-                    s1p[:].rearrange("p (t m) -> p t m", t=PACK), s1.rearrange("p (m t) -> p t m", t=PACK)
-                )
-            gs = feed.tile([P, C], U8, name="gs", bufs=3, align_bytes=64)
-            nc.vector.tensor_copy(gs[:], xs[:].indirect(lists))
-            gw = feed.tile([P, C], U32, name="gw", bufs=2, align_bytes=64)
-            nc.vector.tensor_copy(gw[:], xw[:].indirect(lists))
-            if e not in TURNED:
-                hidden[e] = work.tile([P, C * PACK], BF16, name="h", bufs=2, align_bytes=64)
+                hidden[e] = work.tile([P, C * PACK], BF16, name="h", align_bytes=64)
             by_slot[e] = []
             for half in range(C // HALF):
                 cols = slice(half * HALF, (half + 1) * HALF)
                 bank = psum1.tile([P, H], F32, name="bank1")
-                if e in TURNED:
+                if e < HOT:
                     nc.tensor.matmul_mx(
                         out=bank[:], lhsT=gw[:, cols].bitcast(FP8X4), lhsT_scale=gs[:, cols],
-                        rhs=w1.bitcast(fmt), rhs_scale=s1, start=True, stop=True,
+                        rhs=w1h[e][:].bitcast(FP8X4), rhs_scale=s1h[4 * e : P, :], start=True, stop=True,
                     )
-                    hb = work.tile([P, H], BF16, name="hb", bufs=2, align_bytes=64)
+                    hb = work.tile([P, H], BF16, name="hb", align_bytes=64)
                     nc.scalar.activation(
                         hb[:].rearrange("s (u p c) -> s u p c", u=2, c=2),
                         bank[:].rearrange("s (p u c) -> s u p c", u=2, c=2),
@@ -158,8 +148,8 @@ def tile_moe_hot_s_mlp_gelu_kernel(
                     for t in range(PACK):
                         nc.tensor.matmul_mx(
                             out=bank[:, t * HALF : (t + 1) * HALF],
-                            lhsT=w1p[:, 2 * P * t : 2 * P * (t + 1)].bitcast(fmt),
-                            lhsT_scale=s1p[:, P * t : P * (t + 1)],
+                            lhsT=w1p[:, 2 * P * t : 2 * P * (t + 1)].bitcast(FP4X4),
+                            lhsT_scale=s1c[:, e - HOT, P * t : P * (t + 1)],
                             rhs=gw[:, cols].bitcast(FP8X4), rhs_scale=gs[:, cols], start=True, stop=True,
                         )
                     nc.scalar.activation(
@@ -169,23 +159,20 @@ def tile_moe_hot_s_mlp_gelu_kernel(
                     )
 
         def turn(e):
-            bank = psumt.tile([P, C // HALF, 2, HALF], F32, name="bankt")
+            bank = psum2.tile([P, C // HALF, 2, HALF], F32, name="bank2")
             for half in range(C // HALF):
                 words = by_slot[e][half][:].bitcast(F32)
                 for u in range(2):
                     nc.tensor.transpose(bank[:, half, u, :], words[:, u * P : (u + 1) * P], ident[:])
-            hidden[e] = work.tile([P, C * PACK], BF16, name="h", bufs=2, align_bytes=64)
+            hidden[e] = work.tile([P, C * PACK], BF16, name="h", align_bytes=64)
             h_words = hidden[e][:].bitcast(F32).rearrange("p (j s u) -> p j s u", s=HALF, u=2)
-            if e < HOT:
-                nc.vector.tensor_copy(h_words, bank[:].rearrange("p j u s -> p j s u"))
-            else:
-                nc.scalar.copy(h_words, bank[:].rearrange("p j u s -> p j s u"))
+            nc.scalar.copy(h_words, bank[:].rearrange("p j u s -> p j s u"))
 
         def second_layer(unit):
             e, halves = UNITS[unit]
             width = len(halves) * HALF
-            hw = work.tile([P, width], U32, name="hw", bufs=5, align_bytes=64)
-            hs = work.tile([P, width], U8, name="hs", bufs=5, align_bytes=64)
+            hw = work.tile([P, width], U32, name="hw", align_bytes=64)
+            hs = work.tile([P, width], U8, name="hs", align_bytes=64)
             nc.vector.quantize_mx(out=hw[:].bitcast(FP8X4), scales=hs[:], in_=hidden[e][:, halves[0] * H : (halves[-1] + 1) * H])
             bank = psum2.tile([P, N // P, width], F32, name="bank2")
             for a in range(N // P):
@@ -199,7 +186,7 @@ def tile_moe_hot_s_mlp_gelu_kernel(
                     out=bank[:, a, :], lhsT=lhs, lhsT_scale=lhs_s,
                     rhs=hw[:].bitcast(FP8X4), rhs_scale=hs[:], start=True, stop=True,
                 )
-            y = work.tile([P, N // P, width], F32, name="y")
+            y = work.tile([P, N // P, width], F32, name="y", bufs=6)
             if unit in OUTS_ON_VECTOR:
                 nc.vector.tensor_copy(y[:], bank[:])
             else:
@@ -207,15 +194,10 @@ def tile_moe_hot_s_mlp_gelu_kernel(
             first = e * C + halves[0] * HALF
             nc.sync.dma_start(out_view[:, :, first : first + width], y[:])
 
-        for step in range(len(UNITS) + 2):
+        for step in range(len(UNITS) + LAG):
             if step < E:
-                first_layer(ORDER[step])
-            if 1 <= step <= E and ORDER[step - 1] in TURNED:
-                turn(ORDER[step - 1])
-            if step >= 2:
-                second_layer(step - 2)
-            if step == 1:
-                load_hot_words(nc.sync, w1h[:], w1h_words)
-                load_hot_scales(nc.sync, s1h, w1h_scales)
-                load_hot_words(nc.sync, w2h[:], w2h_words)
-                load_hot_scales(nc.sync, s2h, w2h_scales)
+                first_layer(step)
+            if 1 <= step <= HOT:
+                turn(step - 1)
+            if step >= LAG:
+                second_layer(step - LAG)

@@ -21,7 +21,7 @@ P = 128
 PACK = 4
 HALF = 128
 UNITS = [(e, [0, 1]) for e in range(E - 1)] + [(E - 1, [0]), (E - 1, [1])]
-OUTS_ON_VECTOR = [6, 8, 10]
+OUTS_ON_VECTOR = [1, 3, 4, 5, 6, 8, 10]
 LAG = 2
 FIRST = 3
 
@@ -84,6 +84,18 @@ def tile_moe_hot_s_mlp_gelu_kernel(
         def load_token_scales(queue, q):
             queue.dma_start(xs[32 * q : 32 * q + 4, :].bitcast(I32), x_scales[0, 4 * q : 4 * q + 4, :].bitcast(I32))
 
+        def spread_scales(queue, quadrants):
+            for q in quadrants:
+                queue.dma_start(
+                    s1c[32 * q : 32 * q + 4, :, :].bitcast(I32), s1c_moved[32 * q : 32 * q + 32, :].bitcast(I32)
+                )
+
+        def spread_scales(queue, quadrants):
+            for q in quadrants:
+                queue.dma_start(
+                    s1c[32 * q : 32 * q + 4, :, :].bitcast(I32), s1c_moved[32 * q : 32 * q + 32, :].bitcast(I32)
+                )
+
         nc.sync.dma_start(offsets[:], offs)
         nc.scalar.dma_start(s1c_rows[:].bitcast(I32), w1c_scales.rearrange("f s b n -> (s b) f n").bitcast(I32))
         load_token_scales(nc.scalar, 0)
@@ -99,15 +111,14 @@ def tile_moe_hot_s_mlp_gelu_kernel(
         nc.vector.tensor_copy(
             s1c_moved[:].rearrange("p (t m) -> p t m", t=PACK), s1c_rows[:].rearrange("p (m t) -> p t m", t=PACK)
         )
-        for q in range(4):
-            nc.sync.dma_start(
-                s1c[32 * q : 32 * q + 4, :, :].bitcast(I32), s1c_moved[32 * q : 32 * q + 32, :].bitcast(I32)
-            )
+        spread_scales(nc.scalar, [0, 1])
+        spread_scales(nc.sync, [2, 3])
         nc.sync.dma_start(w2h[:], w2h_words.rearrange("e s p n d -> p (e s) (n d)").bitcast(I32))
-        load_hot_scales(nc.sync, s2h, w2h_scales, range(4))
-        load_cold_words(nc.sync, w1c_rest[:], w1c_words[FIRST:COLD])
+        load_hot_scales(nc.scalar, s2h, w2h_scales, [0, 1])
+        load_hot_scales(nc.sync, s2h, w2h_scales, [2, 3])
         load_cold_words(nc.sync, w2c[:], w2c_words)
         load_cold_scales(nc.sync, s2c, w2c_scales, range(4))
+        load_cold_words(nc.sync, w1c_rest[:], w1c_words[FIRST:COLD])
 
         out_view = out.rearrange("(a p) s -> p a s", p=P)
         by_slot = {}

@@ -21,9 +21,11 @@ P = 128
 PACK = 4
 HALF = 128
 UNITS = [(e, [0, 1]) for e in range(E - 1)] + [(E - 1, [0]), (E - 1, [1])]
-OUTS_ON_VECTOR = [1, 3, 4, 5, 6, 8, 10]
+OUTS_ON_VECTOR = [3, 5, 7, 9]
 LAG = 2
 FIRST = 3
+FRONT = 3
+BACK = 5
 
 
 def tile_moe_hot_s_mlp_gelu_kernel(
@@ -35,8 +37,7 @@ def tile_moe_hot_s_mlp_gelu_kernel(
         held = ctx.enter_context(tc.tile_pool(name="held", bufs=1))
         work = ctx.enter_context(tc.tile_pool(name="work", bufs=4))
         feed = ctx.enter_context(tc.tile_pool(name="feed", bufs=3))
-        psum1 = ctx.enter_context(tc.psum_pool(name="psum1", bufs=4))
-        psum2 = ctx.enter_context(tc.psum_pool(name="psum2", bufs=4))
+        psum = ctx.enter_context(tc.psum_pool(name="psum", bufs=1))
 
         offsets = held.tile([P, E * C // 16], U16, name="offsets")
         xw = held.tile([P, T], U32, name="xw", align_bytes=64)
@@ -56,7 +57,7 @@ def tile_moe_hot_s_mlp_gelu_kernel(
         s1h = held.tile([P, H], U8, name="s1h", align_bytes=64)
         s2h = held.tile([P, N], U8, name="s2h", align_bytes=64)
 
-        nc.gpsimd.memset(xs[:].bitcast(I32), 0)
+        nc.vector.memset(xs[:].bitcast(I32), 0)
         make_identity(nc, ident[:])
         nc.vector.memset(s1h[:].bitcast(I32), 0)
         nc.vector.memset(warm[:], 0.0)
@@ -114,12 +115,13 @@ def tile_moe_hot_s_mlp_gelu_kernel(
         spread_scales(nc.scalar, [0, 1])
         spread_scales(nc.sync, [2, 3])
         nc.sync.dma_start(w2h[:], w2h_words.rearrange("e s p n d -> p (e s) (n d)").bitcast(I32))
-        load_hot_scales(nc.scalar, s2h, w2h_scales, [0, 1])
-        load_hot_scales(nc.sync, s2h, w2h_scales, [2, 3])
+        load_hot_scales(nc.sync, s2h, w2h_scales, range(4))
         load_cold_words(nc.sync, w2c[:], w2c_words)
         load_cold_scales(nc.sync, s2c, w2c_scales, range(4))
         load_cold_words(nc.sync, w1c_rest[:], w1c_words[FIRST:COLD])
 
+        front = [psum.tile([P, H], F32, name="front%d" % r) for r in range(FRONT)]
+        back = [psum.tile([P, H], F32, name="back%d" % r) for r in range(BACK)]
         out_view = out.rearrange("(a p) s -> p a s", p=P)
         by_slot = {}
         hidden = {}
@@ -142,7 +144,7 @@ def tile_moe_hot_s_mlp_gelu_kernel(
             by_slot[e] = []
             for half in range(C // HALF):
                 cols = slice(half * HALF, (half + 1) * HALF)
-                bank = psum1.tile([P, H], F32, name="bank1")
+                bank = front[e % FRONT] if half == 0 else back[e % BACK]
                 if e < HOT:
                     nc.tensor.matmul_mx(
                         out=bank[:], lhsT=gw[:, cols].bitcast(FP8X4), lhsT_scale=gs[:, cols],
@@ -170,14 +172,14 @@ def tile_moe_hot_s_mlp_gelu_kernel(
                     )
 
         def turn(e):
-            bank = psum2.tile([P, C // HALF, 2, HALF], F32, name="bank2")
+            bank = back[BACK - HOT + e][:].rearrange("p (j u s) -> p j u s", u=2, s=HALF)
             for half in range(C // HALF):
                 words = by_slot[e][half][:].bitcast(F32)
                 for u in range(2):
                     nc.tensor.transpose(bank[:, half, u, :], words[:, u * P : (u + 1) * P], ident[:])
             hidden[e] = work.tile([P, C * PACK], BF16, name="h", align_bytes=64)
             h_words = hidden[e][:].bitcast(F32).rearrange("p (j s u) -> p j s u", s=HALF, u=2)
-            nc.scalar.copy(h_words, bank[:].rearrange("p j u s -> p j s u"))
+            nc.scalar.copy(h_words, bank.rearrange("p j u s -> p j s u"))
 
         def second_layer(unit):
             e, halves = UNITS[unit]
@@ -185,7 +187,8 @@ def tile_moe_hot_s_mlp_gelu_kernel(
             hw = work.tile([P, width], U32, name="hw", align_bytes=64)
             hs = work.tile([P, width], U8, name="hs", align_bytes=64)
             nc.vector.quantize_mx(out=hw[:].bitcast(FP8X4), scales=hs[:], in_=hidden[e][:, halves[0] * H : (halves[-1] + 1) * H])
-            bank = psum2.tile([P, N // P, width], F32, name="bank2")
+            whole = back[(unit + 1) % BACK] if unit < E - 2 else back[(unit + 2) % BACK]
+            bank = whole[:, 0 : N // P * width].rearrange("p (a s) -> p a s", s=width)
             for a in range(N // P):
                 if e >= HOT:
                     lhs = w2c[:, e - HOT, 2 * P * a : 2 * P * (a + 1)].bitcast(FP4X4)
@@ -199,9 +202,9 @@ def tile_moe_hot_s_mlp_gelu_kernel(
                 )
             y = work.tile([P, N // P, width], F32, name="y", bufs=6)
             if unit in OUTS_ON_VECTOR:
-                nc.vector.tensor_copy(y[:], bank[:])
+                nc.vector.tensor_copy(y[:], bank)
             else:
-                nc.scalar.copy(y[:], bank[:])
+                nc.scalar.copy(y[:], bank)
             first = e * C + halves[0] * HALF
             nc.sync.dma_start(out_view[:, :, first : first + width], y[:])
 

@@ -135,8 +135,11 @@ def tile_moe_hot_s_mlp_gelu_kernel(
             if e >= HOT:
                 f = e - HOT
                 w1 = w1c_first[:, f, :] if f < FIRST else w1c_rest[:, f - FIRST, :]
-                w1p = feed.tile([P, 2 * H], U8, name="w1p", bufs=8, align_bytes=64)
-                nc.gpsimd.tensor_copy(
+                if f < FIRST:
+                    w1p = feed.tile([P, 2 * H], U8, name="w1p_first", bufs=1, align_bytes=64)
+                else:
+                    w1p = feed.tile([P, 2 * H], U8, name="w1p", bufs=COLD - FIRST, align_bytes=64)
+                (nc.vector if f < FIRST else nc.gpsimd).tensor_copy(
                     w1p[:].bitcast(U16).rearrange("p (t m) -> p t m", t=PACK),
                     w1.bitcast(U16).rearrange("p (m t) -> p t m", t=PACK),
                 )

@@ -21,11 +21,13 @@ P = 128
 PACK = 4
 HALF = 128
 UNITS = [(e, [0, 1]) for e in range(E - 1)] + [(E - 1, [0]), (E - 1, [1])]
-OUTS_ON_VECTOR = [3, 5, 7, 9]
-LAG = 2
+OUTS_ON_VECTOR = [6, 7, 10]
 FIRST = 3
-FRONT = 3
-BACK = 5
+RING = 5
+LAG = 3
+GS = 2
+GW = 5
+WP = 2
 
 
 def tile_moe_hot_s_mlp_gelu_kernel(
@@ -36,7 +38,6 @@ def tile_moe_hot_s_mlp_gelu_kernel(
     with ExitStack() as ctx:
         held = ctx.enter_context(tc.tile_pool(name="held", bufs=1))
         work = ctx.enter_context(tc.tile_pool(name="work", bufs=4))
-        feed = ctx.enter_context(tc.tile_pool(name="feed", bufs=3))
         psum = ctx.enter_context(tc.psum_pool(name="psum", bufs=1))
 
         offsets = held.tile([P, E * C // 16], U16, name="offsets")
@@ -48,32 +49,26 @@ def tile_moe_hot_s_mlp_gelu_kernel(
         w1c_first = held.tile([P, FIRST, 2 * H], U8, name="w1c_first", align_bytes=64)
         w1c_rest = held.tile([P, COLD - FIRST, 2 * H], U8, name="w1c_rest", align_bytes=64)
         s1c_rows = held.tile([P, H], U8, name="s1c_rows", align_bytes=64)
-        s1c_moved = held.tile([P, H], U8, name="s1c_moved", align_bytes=64)
-        s1c = held.tile([P, COLD, H], U8, name="s1c", align_bytes=64)
+        sc_rows = held.tile([P, H + N], U8, name="sc_rows", align_bytes=64)
+        sc = held.tile([P, COLD, H + N], U8, name="sc", align_bytes=64)
         w2c = held.tile([P, COLD, 2 * N], U8, name="w2c", align_bytes=64)
-        s2c = held.tile([P, COLD, N], U8, name="s2c", align_bytes=64)
         w1h = [held.tile([P, H], I32, name="w1h%d" % e, align_bytes=64) for e in range(HOT)]
         w2h = held.tile([P, HOT, N], I32, name="w2h", align_bytes=64)
         s1h = held.tile([P, H], U8, name="s1h", align_bytes=64)
         s2h = held.tile([P, N], U8, name="s2h", align_bytes=64)
+        gs_tiles = [held.tile([P, C], U8, name="gs%d" % r, align_bytes=64) for r in range(GS)]
+        gw_tiles = [held.tile([P, C], U32, name="gw%d" % r, align_bytes=64) for r in range(GW)]
+        w1p_tiles = [held.tile([P, 2 * H], U8, name="w1p%d" % r, align_bytes=64) for r in range(WP)]
 
         nc.vector.memset(xs[:].bitcast(I32), 0)
-        make_identity(nc, ident[:])
         nc.vector.memset(s1h[:].bitcast(I32), 0)
         nc.vector.memset(warm[:], 0.0)
-        nc.vector.memset(s1c[:].rearrange("p e n -> p (e n)").bitcast(I32), 0)
-        nc.vector.memset(s2h[:].bitcast(I32), 0)
-        nc.vector.memset(s2c[:].rearrange("p e n -> p (e n)").bitcast(I32), 0)
+        make_identity(nc, ident[:])
+        nc.gpsimd.memset(s2h[:].bitcast(I32), 0)
+        nc.vector.memset(sc[:].rearrange("p e n -> p (e n)").bitcast(I32), 0)
 
         def load_cold_words(queue, tile, words):
             queue.dma_start(tile.bitcast(I32), words.rearrange("e s p b -> p (e s) b").bitcast(I32))
-
-        def load_cold_scales(queue, tile, scales, quadrants):
-            for q in quadrants:
-                queue.dma_start(
-                    tile[32 * q : 32 * q + 4, :, :].bitcast(I32),
-                    scales[:, 0, 4 * q : 4 * q + 4, :].rearrange("e r n -> r e n").bitcast(I32),
-                )
 
         def load_hot_scales(queue, tile, scales, quadrants):
             for q in quadrants:
@@ -85,117 +80,121 @@ def tile_moe_hot_s_mlp_gelu_kernel(
         def load_token_scales(queue, q):
             queue.dma_start(xs[32 * q : 32 * q + 4, :].bitcast(I32), x_scales[0, 4 * q : 4 * q + 4, :].bitcast(I32))
 
-        def spread_scales(queue, quadrants):
-            for q in quadrants:
-                queue.dma_start(
-                    s1c[32 * q : 32 * q + 4, :, :].bitcast(I32), s1c_moved[32 * q : 32 * q + 32, :].bitcast(I32)
-                )
+        def load_hot_words(queue, e):
+            queue.dma_start(w1h[e][:], w1h_words[e, 0].rearrange("p n d -> p (n d)").bitcast(I32))
 
         def spread_scales(queue, quadrants):
             for q in quadrants:
                 queue.dma_start(
-                    s1c[32 * q : 32 * q + 4, :, :].bitcast(I32), s1c_moved[32 * q : 32 * q + 32, :].bitcast(I32)
+                    sc[32 * q : 32 * q + 4, :, :].bitcast(I32), sc_rows[32 * q : 32 * q + 32, :].bitcast(I32)
                 )
 
         nc.sync.dma_start(offsets[:], offs)
         nc.scalar.dma_start(s1c_rows[:].bitcast(I32), w1c_scales.rearrange("f s b n -> (s b) f n").bitcast(I32))
-        load_token_scales(nc.scalar, 0)
-        load_token_scales(nc.scalar, 1)
-        load_token_scales(nc.sync, 2)
-        load_token_scales(nc.sync, 3)
+        load_token_scales(nc.sync, 0)
+        load_token_scales(nc.scalar, 2)
+        load_token_scales(nc.sync, 1)
+        load_token_scales(nc.scalar, 3)
         nc.sync.dma_start(xw[:].bitcast(I32), x_words[0].rearrange("p t d -> p (t d)").bitcast(I32))
-        load_hot_scales(nc.scalar, s1h, w1h_scales, range(4))
+        nc.scalar.dma_start(sc_rows[:, H:].bitcast(I32), w2c_scales.rearrange("f s b n -> (s b) f n").bitcast(I32))
         nc.scalar.activation(warm_out[:], warm[:], GELU)
-        nc.sync.dma_start(w1h[0][:], w1h_words[0, 0].rearrange("p n d -> p (n d)").bitcast(I32))
-        nc.sync.dma_start(w1h[1][:], w1h_words[1, 0].rearrange("p n d -> p (n d)").bitcast(I32))
+        load_hot_words(nc.sync, 0)
+        load_hot_scales(nc.sync, s1h, w1h_scales, range(4))
+        load_hot_words(nc.sync, 1)
         load_cold_words(nc.sync, w1c_first[:], w1c_words[0:FIRST])
-        nc.vector.tensor_copy(
-            s1c_moved[:].rearrange("p (t m) -> p t m", t=PACK), s1c_rows[:].rearrange("p (m t) -> p t m", t=PACK)
-        )
-        spread_scales(nc.scalar, [0, 1])
-        spread_scales(nc.sync, [2, 3])
-        nc.sync.dma_start(w2h[:], w2h_words.rearrange("e s p n d -> p (e s) (n d)").bitcast(I32))
-        load_hot_scales(nc.sync, s2h, w2h_scales, range(4))
-        load_cold_words(nc.sync, w2c[:], w2c_words)
-        load_cold_scales(nc.sync, s2c, w2c_scales, range(4))
-        load_cold_words(nc.sync, w1c_rest[:], w1c_words[FIRST:COLD])
+        load_hot_scales(nc.gpsimd, s2h, w2h_scales, range(4))
 
-        front = [psum.tile([P, H], F32, name="front%d" % r) for r in range(FRONT)]
-        back = [psum.tile([P, H], F32, name="back%d" % r) for r in range(BACK)]
+        banks = [psum.tile([P, H], F32, name="bank%d" % r) for r in range(RING)]
+        taken = []
         out_view = out.rearrange("(a p) s -> p a s", p=P)
         by_slot = {}
         hidden = {}
+        packed = {}
 
-        def first_layer(e):
-            lists = offsets[:, e * C // 16 : (e + 1) * C // 16]
-            gs = feed.tile([P, C], U8, name="gs", bufs=2, align_bytes=64)
-            nc.vector.tensor_copy(gs[:], xs[:].indirect(lists))
-            gw = feed.tile([P, C], U32, name="gw", align_bytes=64)
-            nc.vector.tensor_copy(gw[:], xw[:].indirect(lists))
-            if e >= HOT:
-                f = e - HOT
-                w1 = w1c_first[:, f, :] if f < FIRST else w1c_rest[:, f - FIRST, :]
-                if f < FIRST:
-                    w1p = feed.tile([P, 2 * H], U8, name="w1p_first", bufs=1, align_bytes=64)
-                else:
-                    w1p = feed.tile([P, 2 * H], U8, name="w1p", bufs=COLD - FIRST, align_bytes=64)
-                (nc.vector if f < FIRST else nc.gpsimd).tensor_copy(
-                    w1p[:].bitcast(U16).rearrange("p (t m) -> p t m", t=PACK),
-                    w1.bitcast(U16).rearrange("p (m t) -> p t m", t=PACK),
+        def next_bank():
+            taken.append(len(taken) % RING)
+            return banks[taken[-1]]
+
+        def lists(e):
+            return offsets[:, e * C // 16 : (e + 1) * C // 16]
+
+        def gs(e):
+            return gs_tiles[e % GS]
+
+        def gw(e):
+            return gw_tiles[e % GW]
+
+        def gather_scales(e):
+            nc.vector.tensor_copy(gs(e)[:], xs[:].indirect(lists(e)))
+
+        def gather_words(e):
+            nc.vector.tensor_copy(gw(e)[:], xw[:].indirect(lists(e)))
+
+        def permute(e):
+            f = e - HOT
+            w1 = w1c_first[:, f, :] if f < FIRST else w1c_rest[:, f - FIRST, :]
+            nc.vector.tensor_copy(
+                w1p_tiles[e % WP][:].bitcast(U16).rearrange("p (t m) -> p t m", t=PACK),
+                w1.bitcast(U16).rearrange("p (m t) -> p t m", t=PACK),
+            )
+
+        def first_layer(e, half):
+            cols = slice(half * HALF, (half + 1) * HALF)
+            bank = next_bank()
+            if e < HOT:
+                nc.tensor.matmul_mx(
+                    out=bank[:], lhsT=gw(e)[:, cols].bitcast(FP8X4), lhsT_scale=gs(e)[:, cols],
+                    rhs=w1h[e][:].bitcast(FP8X4), rhs_scale=s1h[4 * e : P, :], start=True, stop=True,
                 )
-                hidden[e] = work.tile([P, C * PACK], BF16, name="h", align_bytes=64)
-            by_slot[e] = []
-            for half in range(C // HALF):
-                cols = slice(half * HALF, (half + 1) * HALF)
-                bank = front[e % FRONT] if half == 0 else back[e % BACK]
-                if e < HOT:
+                by_slot[e, half] = work.tile([P, H], BF16, name="hb", align_bytes=64)
+                nc.scalar.activation(
+                    by_slot[e, half][:].rearrange("s (u p c) -> s u p c", u=2, c=2),
+                    bank[:].rearrange("s (p u c) -> s u p c", u=2, c=2),
+                    GELU,
+                )
+            else:
+                if half == 0:
+                    hidden[e] = work.tile([P, C * PACK], BF16, name="h", align_bytes=64)
+                for t in range(PACK):
                     nc.tensor.matmul_mx(
-                        out=bank[:], lhsT=gw[:, cols].bitcast(FP8X4), lhsT_scale=gs[:, cols],
-                        rhs=w1h[e][:].bitcast(FP8X4), rhs_scale=s1h[4 * e : P, :], start=True, stop=True,
+                        out=bank[:, t * HALF : (t + 1) * HALF],
+                        lhsT=w1p_tiles[e % WP][:, 2 * P * t : 2 * P * (t + 1)].bitcast(FP4X4),
+                        lhsT_scale=sc[:, e - HOT, P * t : P * (t + 1)],
+                        rhs=gw(e)[:, cols].bitcast(FP8X4), rhs_scale=gs(e)[:, cols], start=True, stop=True,
                     )
-                    hb = work.tile([P, H], BF16, name="hb", align_bytes=64)
-                    nc.scalar.activation(
-                        hb[:].rearrange("s (u p c) -> s u p c", u=2, c=2),
-                        bank[:].rearrange("s (p u c) -> s u p c", u=2, c=2),
-                        GELU,
-                    )
-                    by_slot[e].append(hb)
-                else:
-                    for t in range(PACK):
-                        nc.tensor.matmul_mx(
-                            out=bank[:, t * HALF : (t + 1) * HALF],
-                            lhsT=w1p[:, 2 * P * t : 2 * P * (t + 1)].bitcast(FP4X4),
-                            lhsT_scale=s1c[:, e - HOT, P * t : P * (t + 1)],
-                            rhs=gw[:, cols].bitcast(FP8X4), rhs_scale=gs[:, cols], start=True, stop=True,
-                        )
-                    nc.scalar.activation(
-                        hidden[e][:, half * H : (half + 1) * H].rearrange("p (s t) -> p s t", t=PACK),
-                        bank[:].rearrange("p (t s) -> p s t", t=PACK),
-                        GELU,
-                    )
+                nc.scalar.activation(
+                    hidden[e][:, half * H : (half + 1) * H].rearrange("p (s t) -> p s t", t=PACK),
+                    bank[:].rearrange("p (t s) -> p s t", t=PACK),
+                    GELU,
+                )
 
         def turn(e):
-            bank = back[BACK - HOT + e][:].rearrange("p (j u s) -> p j u s", u=2, s=HALF)
+            bank = next_bank()[:].rearrange("p (j u s) -> p j u s", u=2, s=HALF)
             for half in range(C // HALF):
-                words = by_slot[e][half][:].bitcast(F32)
+                words = by_slot[e, half][:].bitcast(F32)
                 for u in range(2):
                     nc.tensor.transpose(bank[:, half, u, :], words[:, u * P : (u + 1) * P], ident[:])
             hidden[e] = work.tile([P, C * PACK], BF16, name="h", align_bytes=64)
             h_words = hidden[e][:].bitcast(F32).rearrange("p (j s u) -> p j s u", s=HALF, u=2)
             nc.scalar.copy(h_words, bank.rearrange("p j u s -> p j s u"))
 
-        def second_layer(unit):
+        def quantise(unit):
             e, halves = UNITS[unit]
             width = len(halves) * HALF
             hw = work.tile([P, width], U32, name="hw", align_bytes=64)
             hs = work.tile([P, width], U8, name="hs", align_bytes=64)
             nc.vector.quantize_mx(out=hw[:].bitcast(FP8X4), scales=hs[:], in_=hidden[e][:, halves[0] * H : (halves[-1] + 1) * H])
-            whole = back[(unit + 1) % BACK] if unit < E - 2 else back[(unit + 2) % BACK]
-            bank = whole[:, 0 : N // P * width].rearrange("p (a s) -> p a s", s=width)
+            packed[unit] = (hw, hs)
+
+        def second_layer(unit):
+            e, halves = UNITS[unit]
+            width = len(halves) * HALF
+            hw, hs = packed[unit]
+            bank = next_bank()[:, 0 : N // P * width].rearrange("p (a s) -> p a s", s=width)
             for a in range(N // P):
                 if e >= HOT:
                     lhs = w2c[:, e - HOT, 2 * P * a : 2 * P * (a + 1)].bitcast(FP4X4)
-                    lhs_s = s2c[:, e - HOT, P * a : P * (a + 1)]
+                    lhs_s = sc[:, e - HOT, H + P * a : H + P * (a + 1)]
                 else:
                     lhs = w2h[:, e, P * a : P * (a + 1)].bitcast(FP8X4)
                     lhs_s = s2h[4 * e : P, P * a : P * (a + 1)]
@@ -211,10 +210,48 @@ def tile_moe_hot_s_mlp_gelu_kernel(
             first = e * C + halves[0] * HALF
             nc.sync.dma_start(out_view[:, :, first : first + width], y[:])
 
-        for step in range(len(UNITS) + LAG):
-            if step < E:
-                first_layer(step)
-            if 1 <= step <= HOT:
-                turn(step - 1)
-            if step >= LAG:
-                second_layer(step - LAG)
+        nc.vector.tensor_copy(
+            sc_rows[:, 0:H].rearrange("p (t m) -> p t m", t=PACK), s1c_rows[:].rearrange("p (m t) -> p t m", t=PACK)
+        )
+        spread_scales(nc.sync, [0, 2, 1, 3])
+        nc.sync.dma_start(w2h[:], w2h_words.rearrange("e s p n d -> p (e s) (n d)").bitcast(I32))
+        load_cold_words(nc.sync, w1c_rest[:], w1c_words[FIRST:COLD])
+        load_cold_words(nc.sync, w2c[:], w2c_words)
+
+        gather_scales(0)
+        gather_scales(1)
+        gather_words(0)
+        gather_words(1)
+        first_layer(0, 0)
+        first_layer(0, 1)
+        first_layer(1, 0)
+        turn(0)
+        first_layer(1, 1)
+        gather_scales(2)
+        permute(2)
+        for e in range(HOT, E):
+            gather_words(e)
+            if e == E - 1:
+                second_layer(e - LAG)
+            first_layer(e, 0)
+            first_layer(e, 1)
+            if e == HOT:
+                turn(1)
+            if e + 1 < E:
+                gather_scales(e + 1)
+                permute(e + 1)
+            if e == HOT + 1:
+                quantise(0)
+            if e == HOT + 2:
+                quantise(1)
+            if e >= HOT + 2:
+                quantise(e - 2)
+            if LAG <= e < E - 1:
+                second_layer(e - LAG)
+        quantise(E - 2)
+        second_layer(E - 3)
+        quantise(E - 1)
+        second_layer(E - 2)
+        quantise(E)
+        second_layer(E - 1)
+        second_layer(E)

@@ -22,12 +22,13 @@ PACK = 4
 HALF = 128
 UNITS = [(e, [0, 1]) for e in range(E - 1)] + [(E - 1, [0]), (E - 1, [1])]
 OUTS_ON_VECTOR = [6, 7, 10]
-FIRST = 3
+LOADS = [(0, 2), (2, 5), (5, 8)]
 RING = 5
 LAG = 3
+ON_GPSIMD = 5
 GS = 2
-GW = 5
-WP = 2
+GW = 4
+WP = 6
 
 
 def tile_moe_hot_s_mlp_gelu_kernel(
@@ -46,11 +47,11 @@ def tile_moe_hot_s_mlp_gelu_kernel(
         ident = held.tile([P, P], F32, name="ident")
         warm = held.tile([P, 16], F32, name="warm")
         warm_out = held.tile([P, 16], BF16, name="warm_out")
-        w1c_first = held.tile([P, FIRST, 2 * H], U8, name="w1c_first", align_bytes=64)
-        w1c_rest = held.tile([P, COLD - FIRST, 2 * H], U8, name="w1c_rest", align_bytes=64)
+        w1c = [held.tile([P, b - a, 2 * H], U8, name="w1c%d" % a, align_bytes=64) for a, b in LOADS]
         s1c_rows = held.tile([P, H], U8, name="s1c_rows", align_bytes=64)
-        sc_rows = held.tile([P, H + N], U8, name="sc_rows", align_bytes=64)
-        sc = held.tile([P, COLD, H + N], U8, name="sc", align_bytes=64)
+        s1c_moved = held.tile([P, H], U8, name="s1c_moved", align_bytes=64)
+        s1c = held.tile([P, COLD, H], U8, name="s1c", align_bytes=64)
+        s2c = held.tile([P, COLD, N], U8, name="s2c", align_bytes=64)
         w2c = held.tile([P, COLD, 2 * N], U8, name="w2c", align_bytes=64)
         w1h = [held.tile([P, H], I32, name="w1h%d" % e, align_bytes=64) for e in range(HOT)]
         w2h = held.tile([P, HOT, N], I32, name="w2h", align_bytes=64)
@@ -62,10 +63,11 @@ def tile_moe_hot_s_mlp_gelu_kernel(
 
         nc.vector.memset(xs[:].bitcast(I32), 0)
         nc.vector.memset(s1h[:].bitcast(I32), 0)
+        nc.vector.memset(s2c[:].rearrange("p e n -> p (e n)").bitcast(I32), 0)
         nc.vector.memset(warm[:], 0.0)
         make_identity(nc, ident[:])
-        nc.gpsimd.memset(s2h[:].bitcast(I32), 0)
-        nc.vector.memset(sc[:].rearrange("p e n -> p (e n)").bitcast(I32), 0)
+        nc.vector.memset(s1c[:].rearrange("p e n -> p (e n)").bitcast(I32), 0)
+        nc.vector.memset(s2h[:].bitcast(I32), 0)
 
         def load_cold_words(queue, tile, words):
             queue.dma_start(tile.bitcast(I32), words.rearrange("e s p b -> p (e s) b").bitcast(I32))
@@ -86,7 +88,7 @@ def tile_moe_hot_s_mlp_gelu_kernel(
         def spread_scales(queue, quadrants):
             for q in quadrants:
                 queue.dma_start(
-                    sc[32 * q : 32 * q + 4, :, :].bitcast(I32), sc_rows[32 * q : 32 * q + 32, :].bitcast(I32)
+                    s1c[32 * q : 32 * q + 4, :, :].bitcast(I32), s1c_moved[32 * q : 32 * q + 32, :].bitcast(I32)
                 )
 
         nc.sync.dma_start(offsets[:], offs)
@@ -96,13 +98,15 @@ def tile_moe_hot_s_mlp_gelu_kernel(
         load_token_scales(nc.sync, 1)
         load_token_scales(nc.scalar, 3)
         nc.sync.dma_start(xw[:].bitcast(I32), x_words[0].rearrange("p t d -> p (t d)").bitcast(I32))
-        nc.scalar.dma_start(sc_rows[:, H:].bitcast(I32), w2c_scales.rearrange("f s b n -> (s b) f n").bitcast(I32))
+        load_hot_scales(nc.scalar, s1h, w1h_scales, range(4))
         nc.scalar.activation(warm_out[:], warm[:], GELU)
         load_hot_words(nc.sync, 0)
-        load_hot_scales(nc.sync, s1h, w1h_scales, range(4))
         load_hot_words(nc.sync, 1)
-        load_cold_words(nc.sync, w1c_first[:], w1c_words[0:FIRST])
-        load_hot_scales(nc.gpsimd, s2h, w2h_scales, range(4))
+        load_cold_words(nc.sync, w1c[0][:], w1c_words[slice(*LOADS[0])])
+        for r in range(4):
+            nc.gpsimd.dma_start(
+                s2c[r:P:32, :, :].bitcast(I32), w2c_scales[:, 0, r:16:4, :].rearrange("e q n -> q e n").bitcast(I32)
+            )
 
         banks = [psum.tile([P, H], F32, name="bank%d" % r) for r in range(RING)]
         taken = []
@@ -132,8 +136,8 @@ def tile_moe_hot_s_mlp_gelu_kernel(
 
         def permute(e):
             f = e - HOT
-            w1 = w1c_first[:, f, :] if f < FIRST else w1c_rest[:, f - FIRST, :]
-            nc.vector.tensor_copy(
+            w1 = [tile[:, f - a, :] for tile, (a, b) in zip(w1c, LOADS) if a <= f < b][0]
+            (nc.gpsimd if f < ON_GPSIMD else nc.vector).tensor_copy(
                 w1p_tiles[e % WP][:].bitcast(U16).rearrange("p (t m) -> p t m", t=PACK),
                 w1.bitcast(U16).rearrange("p (m t) -> p t m", t=PACK),
             )
@@ -159,7 +163,7 @@ def tile_moe_hot_s_mlp_gelu_kernel(
                     nc.tensor.matmul_mx(
                         out=bank[:, t * HALF : (t + 1) * HALF],
                         lhsT=w1p_tiles[e % WP][:, 2 * P * t : 2 * P * (t + 1)].bitcast(FP4X4),
-                        lhsT_scale=sc[:, e - HOT, P * t : P * (t + 1)],
+                        lhsT_scale=s1c[:, e - HOT, P * t : P * (t + 1)],
                         rhs=gw(e)[:, cols].bitcast(FP8X4), rhs_scale=gs(e)[:, cols], start=True, stop=True,
                     )
                 nc.scalar.activation(
@@ -194,7 +198,7 @@ def tile_moe_hot_s_mlp_gelu_kernel(
             for a in range(N // P):
                 if e >= HOT:
                     lhs = w2c[:, e - HOT, 2 * P * a : 2 * P * (a + 1)].bitcast(FP4X4)
-                    lhs_s = sc[:, e - HOT, H + P * a : H + P * (a + 1)]
+                    lhs_s = s2c[:, e - HOT, P * a : P * (a + 1)]
                 else:
                     lhs = w2h[:, e, P * a : P * (a + 1)].bitcast(FP8X4)
                     lhs_s = s2h[4 * e : P, P * a : P * (a + 1)]
@@ -211,12 +215,15 @@ def tile_moe_hot_s_mlp_gelu_kernel(
             nc.sync.dma_start(out_view[:, :, first : first + width], y[:])
 
         nc.vector.tensor_copy(
-            sc_rows[:, 0:H].rearrange("p (t m) -> p t m", t=PACK), s1c_rows[:].rearrange("p (m t) -> p t m", t=PACK)
+            s1c_moved[:].rearrange("p (t m) -> p t m", t=PACK), s1c_rows[:].rearrange("p (m t) -> p t m", t=PACK)
         )
-        spread_scales(nc.sync, [0, 2, 1, 3])
+        spread_scales(nc.scalar, [0, 1])
+        spread_scales(nc.sync, [2, 3])
+        load_cold_words(nc.sync, w1c[1][:], w1c_words[slice(*LOADS[1])])
         nc.sync.dma_start(w2h[:], w2h_words.rearrange("e s p n d -> p (e s) (n d)").bitcast(I32))
-        load_cold_words(nc.sync, w1c_rest[:], w1c_words[FIRST:COLD])
+        load_hot_scales(nc.sync, s2h, w2h_scales, range(4))
         load_cold_words(nc.sync, w2c[:], w2c_words)
+        load_cold_words(nc.sync, w1c[2][:], w1c_words[slice(*LOADS[2])])
 
         gather_scales(0)
         gather_scales(1)
@@ -227,6 +234,7 @@ def tile_moe_hot_s_mlp_gelu_kernel(
         first_layer(1, 0)
         turn(0)
         first_layer(1, 1)
+        turn(1)
         gather_scales(2)
         permute(2)
         for e in range(HOT, E):
@@ -235,8 +243,6 @@ def tile_moe_hot_s_mlp_gelu_kernel(
                 second_layer(e - LAG)
             first_layer(e, 0)
             first_layer(e, 1)
-            if e == HOT:
-                turn(1)
             if e + 1 < E:
                 gather_scales(e + 1)
                 permute(e + 1)

@@ -21,13 +21,14 @@ P = 128
 PACK = 4
 HALF = 128
 UNITS = [(e, [0, 1]) for e in range(E - 1)] + [(E - 1, [0]), (E - 1, [1])]
-OUTS_ON_VECTOR = [6, 7, 10]
+OUTS_ON_VECTOR = [4, 6, 7, 10]
 LOADS = [(0, 2), (2, 5), (5, 8)]
 RING = 5
 LAG = 3
+TURN_AT = 1
 ON_GPSIMD = 5
 GS = 2
-GW = 4
+GW = 5
 WP = 6
 
 
@@ -234,7 +235,8 @@ def tile_moe_hot_s_mlp_gelu_kernel(
         first_layer(1, 0)
         turn(0)
         first_layer(1, 1)
-        turn(1)
+        if TURN_AT == 0:
+            turn(1)
         gather_scales(2)
         permute(2)
         for e in range(HOT, E):
@@ -242,7 +244,11 @@ def tile_moe_hot_s_mlp_gelu_kernel(
             if e == E - 1:
                 second_layer(e - LAG)
             first_layer(e, 0)
+            if e == HOT and TURN_AT == 1:
+                turn(1)
             first_layer(e, 1)
+            if e == HOT and TURN_AT == 2:
+                turn(1)
             if e + 1 < E:
                 gather_scales(e + 1)
                 permute(e + 1)

@@ -19,17 +19,20 @@ GELU = mybir.ActivationFunctionType.Gelu_apprx_tanh
 
 P = 128
 PACK = 4
+QUAD = 32
 HALF = 128
 UNITS = [(e, [0, 1]) for e in range(E - 1)] + [(E - 1, [0]), (E - 1, [1])]
-OUTS_ON_VECTOR = [4, 6, 7, 10]
-LOADS = [(0, 2), (2, 5), (5, 8)]
-RING = 5
 LAG = 3
-TURN_AT = 1
+BALANCE_UNIT = 4
+OUTS_ON_VECTOR = [BALANCE_UNIT, E - LAG - 1, E - LAG, E]
 ON_GPSIMD = 5
-GS = 2
-GW = 5
-WP = 6
+W1C_LOADS = [(0, 2), (2, ON_GPSIMD), (ON_GPSIMD, COLD)]
+RING = 5
+SCALE_TILES = 2
+WORD_TILES = 5
+W1P_TILES = ON_GPSIMD + 1
+WORK_BUFS = LAG + 1
+Y_BUFS = 6
 
 
 def tile_moe_hot_s_mlp_gelu_kernel(
@@ -39,16 +42,14 @@ def tile_moe_hot_s_mlp_gelu_kernel(
     nc = tc.nc
     with ExitStack() as ctx:
         held = ctx.enter_context(tc.tile_pool(name="held", bufs=1))
-        work = ctx.enter_context(tc.tile_pool(name="work", bufs=4))
+        work = ctx.enter_context(tc.tile_pool(name="work", bufs=WORK_BUFS))
         psum = ctx.enter_context(tc.psum_pool(name="psum", bufs=1))
 
         offsets = held.tile([P, E * C // 16], U16, name="offsets")
         xw = held.tile([P, T], U32, name="xw", align_bytes=64)
         xs = held.tile([P, T], U8, name="xs", align_bytes=64)
         ident = held.tile([P, P], F32, name="ident")
-        warm = held.tile([P, 16], F32, name="warm")
-        warm_out = held.tile([P, 16], BF16, name="warm_out")
-        w1c = [held.tile([P, b - a, 2 * H], U8, name="w1c%d" % a, align_bytes=64) for a, b in LOADS]
+        w1c = [held.tile([P, b - a, 2 * H], U8, name="w1c%d" % a, align_bytes=64) for a, b in W1C_LOADS]
         s1c_rows = held.tile([P, H], U8, name="s1c_rows", align_bytes=64)
         s1c_moved = held.tile([P, H], U8, name="s1c_moved", align_bytes=64)
         s1c = held.tile([P, COLD, H], U8, name="s1c", align_bytes=64)
@@ -58,14 +59,13 @@ def tile_moe_hot_s_mlp_gelu_kernel(
         w2h = held.tile([P, HOT, N], I32, name="w2h", align_bytes=64)
         s1h = held.tile([P, H], U8, name="s1h", align_bytes=64)
         s2h = held.tile([P, N], U8, name="s2h", align_bytes=64)
-        gs_tiles = [held.tile([P, C], U8, name="gs%d" % r, align_bytes=64) for r in range(GS)]
-        gw_tiles = [held.tile([P, C], U32, name="gw%d" % r, align_bytes=64) for r in range(GW)]
-        w1p_tiles = [held.tile([P, 2 * H], U8, name="w1p%d" % r, align_bytes=64) for r in range(WP)]
+        gs_tiles = [held.tile([P, C], U8, name="gs%d" % r, align_bytes=64) for r in range(SCALE_TILES)]
+        gw_tiles = [held.tile([P, C], U32, name="gw%d" % r, align_bytes=64) for r in range(WORD_TILES)]
+        w1p_tiles = [held.tile([P, 2 * H], U8, name="w1p%d" % r, align_bytes=64) for r in range(W1P_TILES)]
 
         nc.vector.memset(xs[:].bitcast(I32), 0)
         nc.vector.memset(s1h[:].bitcast(I32), 0)
         nc.vector.memset(s2c[:].rearrange("p e n -> p (e n)").bitcast(I32), 0)
-        nc.vector.memset(warm[:], 0.0)
         make_identity(nc, ident[:])
         nc.vector.memset(s1c[:].rearrange("p e n -> p (e n)").bitcast(I32), 0)
         nc.vector.memset(s2h[:].bitcast(I32), 0)
@@ -73,23 +73,29 @@ def tile_moe_hot_s_mlp_gelu_kernel(
         def load_cold_words(queue, tile, words):
             queue.dma_start(tile.bitcast(I32), words.rearrange("e s p b -> p (e s) b").bitcast(I32))
 
-        def load_hot_scales(queue, tile, scales, quadrants):
-            for q in quadrants:
+        def load_cold_w1(part):
+            load_cold_words(nc.sync, w1c[part][:], w1c_words[slice(*W1C_LOADS[part])])
+
+        def load_hot_scales(queue, tile, scales):
+            for q in range(4):
                 queue.dma_start(
-                    tile[32 * q : 32 * q + 4 * HOT, :].bitcast(I32),
+                    tile[QUAD * q : QUAD * q + 4 * HOT, :].bitcast(I32),
                     scales[:, 0, 4 * q : 4 * q + 4, :].bitcast(I32),
                 )
 
         def load_token_scales(queue, q):
-            queue.dma_start(xs[32 * q : 32 * q + 4, :].bitcast(I32), x_scales[0, 4 * q : 4 * q + 4, :].bitcast(I32))
+            queue.dma_start(
+                xs[QUAD * q : QUAD * q + 4, :].bitcast(I32), x_scales[0, 4 * q : 4 * q + 4, :].bitcast(I32)
+            )
 
-        def load_hot_words(queue, e):
-            queue.dma_start(w1h[e][:], w1h_words[e, 0].rearrange("p n d -> p (n d)").bitcast(I32))
+        def load_hot_w1(e):
+            nc.sync.dma_start(w1h[e][:], w1h_words[e, 0].rearrange("p n d -> p (n d)").bitcast(I32))
 
         def spread_scales(queue, quadrants):
             for q in quadrants:
                 queue.dma_start(
-                    s1c[32 * q : 32 * q + 4, :, :].bitcast(I32), s1c_moved[32 * q : 32 * q + 32, :].bitcast(I32)
+                    s1c[QUAD * q : QUAD * q + 4, :, :].bitcast(I32),
+                    s1c_moved[QUAD * q : QUAD * q + QUAD, :].bitcast(I32),
                 )
 
         nc.sync.dma_start(offsets[:], offs)
@@ -99,14 +105,14 @@ def tile_moe_hot_s_mlp_gelu_kernel(
         load_token_scales(nc.sync, 1)
         load_token_scales(nc.scalar, 3)
         nc.sync.dma_start(xw[:].bitcast(I32), x_words[0].rearrange("p t d -> p (t d)").bitcast(I32))
-        load_hot_scales(nc.scalar, s1h, w1h_scales, range(4))
-        nc.scalar.activation(warm_out[:], warm[:], GELU)
-        load_hot_words(nc.sync, 0)
-        load_hot_words(nc.sync, 1)
-        load_cold_words(nc.sync, w1c[0][:], w1c_words[slice(*LOADS[0])])
+        load_hot_scales(nc.scalar, s1h, w1h_scales)
+        load_hot_w1(0)
+        load_hot_w1(1)
+        load_cold_w1(0)
         for r in range(4):
             nc.gpsimd.dma_start(
-                s2c[r:P:32, :, :].bitcast(I32), w2c_scales[:, 0, r:16:4, :].rearrange("e q n -> q e n").bitcast(I32)
+                s2c[r:P:QUAD, :, :].bitcast(I32),
+                w2c_scales[:, 0, r:16:4, :].rearrange("e q n -> q e n").bitcast(I32),
             )
 
         banks = [psum.tile([P, H], F32, name="bank%d" % r) for r in range(RING)]
@@ -124,10 +130,10 @@ def tile_moe_hot_s_mlp_gelu_kernel(
             return offsets[:, e * C // 16 : (e + 1) * C // 16]
 
         def gs(e):
-            return gs_tiles[e % GS]
+            return gs_tiles[e % SCALE_TILES]
 
         def gw(e):
-            return gw_tiles[e % GW]
+            return gw_tiles[e % WORD_TILES]
 
         def gather_scales(e):
             nc.vector.tensor_copy(gs(e)[:], xs[:].indirect(lists(e)))
@@ -137,9 +143,9 @@ def tile_moe_hot_s_mlp_gelu_kernel(
 
         def permute(e):
             f = e - HOT
-            w1 = [tile[:, f - a, :] for tile, (a, b) in zip(w1c, LOADS) if a <= f < b][0]
+            w1 = [tile[:, f - a, :] for tile, (a, b) in zip(w1c, W1C_LOADS) if a <= f < b][0]
             (nc.gpsimd if f < ON_GPSIMD else nc.vector).tensor_copy(
-                w1p_tiles[e % WP][:].bitcast(U16).rearrange("p (t m) -> p t m", t=PACK),
+                w1p_tiles[e % W1P_TILES][:].bitcast(U16).rearrange("p (t m) -> p t m", t=PACK),
                 w1.bitcast(U16).rearrange("p (m t) -> p t m", t=PACK),
             )
 
@@ -163,7 +169,7 @@ def tile_moe_hot_s_mlp_gelu_kernel(
                 for t in range(PACK):
                     nc.tensor.matmul_mx(
                         out=bank[:, t * HALF : (t + 1) * HALF],
-                        lhsT=w1p_tiles[e % WP][:, 2 * P * t : 2 * P * (t + 1)].bitcast(FP4X4),
+                        lhsT=w1p_tiles[e % W1P_TILES][:, 2 * P * t : 2 * P * (t + 1)].bitcast(FP4X4),
                         lhsT_scale=s1c[:, e - HOT, P * t : P * (t + 1)],
                         rhs=gw(e)[:, cols].bitcast(FP8X4), rhs_scale=gs(e)[:, cols], start=True, stop=True,
                     )
@@ -188,7 +194,9 @@ def tile_moe_hot_s_mlp_gelu_kernel(
             width = len(halves) * HALF
             hw = work.tile([P, width], U32, name="hw", align_bytes=64)
             hs = work.tile([P, width], U8, name="hs", align_bytes=64)
-            nc.vector.quantize_mx(out=hw[:].bitcast(FP8X4), scales=hs[:], in_=hidden[e][:, halves[0] * H : (halves[-1] + 1) * H])
+            nc.vector.quantize_mx(
+                out=hw[:].bitcast(FP8X4), scales=hs[:], in_=hidden[e][:, halves[0] * H : (halves[-1] + 1) * H]
+            )
             packed[unit] = (hw, hs)
 
         def second_layer(unit):
@@ -207,7 +215,7 @@ def tile_moe_hot_s_mlp_gelu_kernel(
                     out=bank[:, a, :], lhsT=lhs, lhsT_scale=lhs_s,
                     rhs=hw[:].bitcast(FP8X4), rhs_scale=hs[:], start=True, stop=True,
                 )
-            y = work.tile([P, N // P, width], F32, name="y", bufs=6)
+            y = work.tile([P, N // P, width], F32, name="y", bufs=Y_BUFS)
             if unit in OUTS_ON_VECTOR:
                 nc.vector.tensor_copy(y[:], bank)
             else:
@@ -220,11 +228,11 @@ def tile_moe_hot_s_mlp_gelu_kernel(
         )
         spread_scales(nc.scalar, [0, 1])
         spread_scales(nc.sync, [2, 3])
-        load_cold_words(nc.sync, w1c[1][:], w1c_words[slice(*LOADS[1])])
+        load_cold_w1(1)
         nc.sync.dma_start(w2h[:], w2h_words.rearrange("e s p n d -> p (e s) (n d)").bitcast(I32))
-        load_hot_scales(nc.sync, s2h, w2h_scales, range(4))
+        load_hot_scales(nc.sync, s2h, w2h_scales)
         load_cold_words(nc.sync, w2c[:], w2c_words)
-        load_cold_words(nc.sync, w1c[2][:], w1c_words[slice(*LOADS[2])])
+        load_cold_w1(2)
 
         gather_scales(0)
         gather_scales(1)
@@ -235,35 +243,26 @@ def tile_moe_hot_s_mlp_gelu_kernel(
         first_layer(1, 0)
         turn(0)
         first_layer(1, 1)
-        if TURN_AT == 0:
-            turn(1)
-        gather_scales(2)
-        permute(2)
+        gather_scales(HOT)
+        permute(HOT)
         for e in range(HOT, E):
             gather_words(e)
             if e == E - 1:
                 second_layer(e - LAG)
             first_layer(e, 0)
-            if e == HOT and TURN_AT == 1:
+            if e == HOT:
                 turn(1)
             first_layer(e, 1)
-            if e == HOT and TURN_AT == 2:
-                turn(1)
             if e + 1 < E:
                 gather_scales(e + 1)
                 permute(e + 1)
-            if e == HOT + 1:
-                quantise(0)
-            if e == HOT + 2:
-                quantise(1)
-            if e >= HOT + 2:
+            if 0 <= e - LAG < HOT:
+                quantise(e - LAG)
+            if e - 2 >= HOT:
                 quantise(e - 2)
             if LAG <= e < E - 1:
                 second_layer(e - LAG)
-        quantise(E - 2)
-        second_layer(E - 3)
-        quantise(E - 1)
-        second_layer(E - 2)
-        quantise(E)
-        second_layer(E - 1)
-        second_layer(E)
+        for unit in range(E - 2, len(UNITS)):
+            quantise(unit)
+            second_layer(unit - 1)
+        second_layer(len(UNITS) - 1)

from contextlib import ExitStack

import concourse.mybir as mybir
from concourse.masks import make_identity

K, T, E, C, H, N, HOT = 512, 1280, 10, 256, 512, 256, 2
COLD = E - HOT
FLOPS = 2 * E * C * (K * H + H * N)

F32 = mybir.dt.float32
BF16 = mybir.dt.bfloat16
I32 = mybir.dt.int32
U32 = mybir.dt.uint32
U16 = mybir.dt.uint16
U8 = mybir.dt.uint8
FP8X4 = mybir.dt.float8_e4m3fn_x4
FP4X4 = mybir.dt.float4_e2m1fn_x4
GELU = mybir.ActivationFunctionType.Gelu_apprx_tanh

P = 128
PACK = 4
QUAD = 32
HALF = 128
UNITS = [(e, [0, 1]) for e in range(E - 1)] + [(E - 1, [0]), (E - 1, [1])]
LAG = 3
BALANCE_UNIT = 4
OUTS_ON_VECTOR = [BALANCE_UNIT, E - LAG - 1, E - LAG, E]
ON_GPSIMD = 5
W1C_LOADS = [(0, 2), (2, ON_GPSIMD), (ON_GPSIMD, COLD)]
RING = 5
SCALE_TILES = 2
WORD_TILES = 5
W1P_TILES = ON_GPSIMD + 1
WORK_BUFS = LAG + 1
Y_BUFS = 6


def tile_moe_hot_s_mlp_gelu_kernel(
    tc, x_words, x_scales, w1h_words, w1h_scales, w2h_words, w2h_scales,
    w1c_words, w1c_scales, w2c_words, w2c_scales, offs, out,
):
    nc = tc.nc
    with ExitStack() as ctx:
        held = ctx.enter_context(tc.tile_pool(name="held", bufs=1))
        work = ctx.enter_context(tc.tile_pool(name="work", bufs=WORK_BUFS))
        psum = ctx.enter_context(tc.psum_pool(name="psum", bufs=1))

        offsets = held.tile([P, E * C // 16], U16, name="offsets")
        xw = held.tile([P, T], U32, name="xw", align_bytes=64)
        xs = held.tile([P, T], U8, name="xs", align_bytes=64)
        ident = held.tile([P, P], F32, name="ident")
        w1c = [held.tile([P, b - a, 2 * H], U8, name="w1c%d" % a, align_bytes=64) for a, b in W1C_LOADS]
        s1c_rows = held.tile([P, H], U8, name="s1c_rows", align_bytes=64)
        s1c_moved = held.tile([P, H], U8, name="s1c_moved", align_bytes=64)
        s1c = held.tile([P, COLD, H], U8, name="s1c", align_bytes=64)
        s2c = held.tile([P, COLD, N], U8, name="s2c", align_bytes=64)
        w2c = held.tile([P, COLD, 2 * N], U8, name="w2c", align_bytes=64)
        w1h = [held.tile([P, H], I32, name="w1h%d" % e, align_bytes=64) for e in range(HOT)]
        w2h = held.tile([P, HOT, N], I32, name="w2h", align_bytes=64)
        s1h = held.tile([P, H], U8, name="s1h", align_bytes=64)
        s2h = held.tile([P, N], U8, name="s2h", align_bytes=64)
        gs_tiles = [held.tile([P, C], U8, name="gs%d" % r, align_bytes=64) for r in range(SCALE_TILES)]
        gw_tiles = [held.tile([P, C], U32, name="gw%d" % r, align_bytes=64) for r in range(WORD_TILES)]
        w1p_tiles = [held.tile([P, 2 * H], U8, name="w1p%d" % r, align_bytes=64) for r in range(W1P_TILES)]

        nc.vector.memset(xs[:].bitcast(I32), 0)
        nc.vector.memset(s1h[:].bitcast(I32), 0)
        nc.vector.memset(s2c[:].rearrange("p e n -> p (e n)").bitcast(I32), 0)
        make_identity(nc, ident[:])
        nc.vector.memset(s1c[:].rearrange("p e n -> p (e n)").bitcast(I32), 0)
        nc.vector.memset(s2h[:].bitcast(I32), 0)

        def load_cold_words(queue, tile, words):
            queue.dma_start(tile.bitcast(I32), words.rearrange("e s p b -> p (e s) b").bitcast(I32))

        def load_cold_w1(part):
            load_cold_words(nc.sync, w1c[part][:], w1c_words[slice(*W1C_LOADS[part])])

        def load_hot_scales(queue, tile, scales):
            for q in range(4):
                queue.dma_start(
                    tile[QUAD * q : QUAD * q + 4 * HOT, :].bitcast(I32),
                    scales[:, 0, 4 * q : 4 * q + 4, :].bitcast(I32),
                )

        def load_token_scales(queue, q):
            queue.dma_start(
                xs[QUAD * q : QUAD * q + 4, :].bitcast(I32), x_scales[0, 4 * q : 4 * q + 4, :].bitcast(I32)
            )

        def load_hot_w1(e):
            nc.sync.dma_start(w1h[e][:], w1h_words[e, 0].rearrange("p n d -> p (n d)").bitcast(I32))

        def spread_scales(queue, quadrants):
            for q in quadrants:
                queue.dma_start(
                    s1c[QUAD * q : QUAD * q + 4, :, :].bitcast(I32),
                    s1c_moved[QUAD * q : QUAD * q + QUAD, :].bitcast(I32),
                )

        nc.sync.dma_start(offsets[:], offs)
        nc.scalar.dma_start(s1c_rows[:].bitcast(I32), w1c_scales.rearrange("f s b n -> (s b) f n").bitcast(I32))
        load_token_scales(nc.sync, 0)
        load_token_scales(nc.scalar, 2)
        load_token_scales(nc.sync, 1)
        load_token_scales(nc.scalar, 3)
        nc.sync.dma_start(xw[:].bitcast(I32), x_words[0].rearrange("p t d -> p (t d)").bitcast(I32))
        load_hot_scales(nc.scalar, s1h, w1h_scales)
        load_hot_w1(0)
        load_hot_w1(1)
        load_cold_w1(0)
        for r in range(4):
            nc.gpsimd.dma_start(
                s2c[r:P:QUAD, :, :].bitcast(I32),
                w2c_scales[:, 0, r:16:4, :].rearrange("e q n -> q e n").bitcast(I32),
            )

        banks = [psum.tile([P, H], F32, name="bank%d" % r) for r in range(RING)]
        taken = []
        out_view = out.rearrange("(a p) s -> p a s", p=P)
        by_slot = {}
        hidden = {}
        packed = {}

        def next_bank():
            taken.append(len(taken) % RING)
            return banks[taken[-1]]

        def lists(e):
            return offsets[:, e * C // 16 : (e + 1) * C // 16]

        def gs(e):
            return gs_tiles[e % SCALE_TILES]

        def gw(e):
            return gw_tiles[e % WORD_TILES]

        def gather_scales(e):
            nc.vector.tensor_copy(gs(e)[:], xs[:].indirect(lists(e)))

        def gather_words(e):
            nc.vector.tensor_copy(gw(e)[:], xw[:].indirect(lists(e)))

        def permute(e):
            f = e - HOT
            w1 = [tile[:, f - a, :] for tile, (a, b) in zip(w1c, W1C_LOADS) if a <= f < b][0]
            (nc.gpsimd if f < ON_GPSIMD else nc.vector).tensor_copy(
                w1p_tiles[e % W1P_TILES][:].bitcast(U16).rearrange("p (t m) -> p t m", t=PACK),
                w1.bitcast(U16).rearrange("p (m t) -> p t m", t=PACK),
            )

        def first_layer(e, half):
            cols = slice(half * HALF, (half + 1) * HALF)
            bank = next_bank()
            if e < HOT:
                nc.tensor.matmul_mx(
                    out=bank[:], lhsT=gw(e)[:, cols].bitcast(FP8X4), lhsT_scale=gs(e)[:, cols],
                    rhs=w1h[e][:].bitcast(FP8X4), rhs_scale=s1h[4 * e : P, :], start=True, stop=True,
                )
                by_slot[e, half] = work.tile([P, H], BF16, name="hb", align_bytes=64)
                nc.scalar.activation(
                    by_slot[e, half][:].rearrange("s (u p c) -> s u p c", u=2, c=2),
                    bank[:].rearrange("s (p u c) -> s u p c", u=2, c=2),
                    GELU,
                )
            else:
                if half == 0:
                    hidden[e] = work.tile([P, C * PACK], BF16, name="h", align_bytes=64)
                for t in range(PACK):
                    nc.tensor.matmul_mx(
                        out=bank[:, t * HALF : (t + 1) * HALF],
                        lhsT=w1p_tiles[e % W1P_TILES][:, 2 * P * t : 2 * P * (t + 1)].bitcast(FP4X4),
                        lhsT_scale=s1c[:, e - HOT, P * t : P * (t + 1)],
                        rhs=gw(e)[:, cols].bitcast(FP8X4), rhs_scale=gs(e)[:, cols], start=True, stop=True,
                    )
                nc.scalar.activation(
                    hidden[e][:, half * H : (half + 1) * H].rearrange("p (s t) -> p s t", t=PACK),
                    bank[:].rearrange("p (t s) -> p s t", t=PACK),
                    GELU,
                )

        def turn(e):
            bank = next_bank()[:].rearrange("p (j u s) -> p j u s", u=2, s=HALF)
            for half in range(C // HALF):
                words = by_slot[e, half][:].bitcast(F32)
                for u in range(2):
                    nc.tensor.transpose(bank[:, half, u, :], words[:, u * P : (u + 1) * P], ident[:])
            hidden[e] = work.tile([P, C * PACK], BF16, name="h", align_bytes=64)
            h_words = hidden[e][:].bitcast(F32).rearrange("p (j s u) -> p j s u", s=HALF, u=2)
            nc.scalar.copy(h_words, bank.rearrange("p j u s -> p j s u"))

        def quantise(unit):
            e, halves = UNITS[unit]
            width = len(halves) * HALF
            hw = work.tile([P, width], U32, name="hw", align_bytes=64)
            hs = work.tile([P, width], U8, name="hs", align_bytes=64)
            nc.vector.quantize_mx(
                out=hw[:].bitcast(FP8X4), scales=hs[:], in_=hidden[e][:, halves[0] * H : (halves[-1] + 1) * H]
            )
            packed[unit] = (hw, hs)

        def second_layer(unit):
            e, halves = UNITS[unit]
            width = len(halves) * HALF
            hw, hs = packed[unit]
            bank = next_bank()[:, 0 : N // P * width].rearrange("p (a s) -> p a s", s=width)
            for a in range(N // P):
                if e >= HOT:
                    lhs = w2c[:, e - HOT, 2 * P * a : 2 * P * (a + 1)].bitcast(FP4X4)
                    lhs_s = s2c[:, e - HOT, P * a : P * (a + 1)]
                else:
                    lhs = w2h[:, e, P * a : P * (a + 1)].bitcast(FP8X4)
                    lhs_s = s2h[4 * e : P, P * a : P * (a + 1)]
                nc.tensor.matmul_mx(
                    out=bank[:, a, :], lhsT=lhs, lhsT_scale=lhs_s,
                    rhs=hw[:].bitcast(FP8X4), rhs_scale=hs[:], start=True, stop=True,
                )
            y = work.tile([P, N // P, width], F32, name="y", bufs=Y_BUFS)
            if unit in OUTS_ON_VECTOR:
                nc.vector.tensor_copy(y[:], bank)
            else:
                nc.scalar.copy(y[:], bank)
            first = e * C + halves[0] * HALF
            nc.sync.dma_start(out_view[:, :, first : first + width], y[:])

        nc.vector.tensor_copy(
            s1c_moved[:].rearrange("p (t m) -> p t m", t=PACK), s1c_rows[:].rearrange("p (m t) -> p t m", t=PACK)
        )
        spread_scales(nc.scalar, [0, 1])
        spread_scales(nc.sync, [2, 3])
        load_cold_w1(1)
        nc.sync.dma_start(w2h[:], w2h_words.rearrange("e s p n d -> p (e s) (n d)").bitcast(I32))
        load_hot_scales(nc.sync, s2h, w2h_scales)
        load_cold_words(nc.sync, w2c[:], w2c_words)
        load_cold_w1(2)

        gather_scales(0)
        gather_scales(1)
        gather_words(0)
        gather_words(1)
        first_layer(0, 0)
        first_layer(0, 1)
        first_layer(1, 0)
        turn(0)
        first_layer(1, 1)
        gather_scales(HOT)
        permute(HOT)
        for e in range(HOT, E):
            gather_words(e)
            if e == E - 1:
                second_layer(e - LAG)
            first_layer(e, 0)
            if e == HOT:
                turn(1)
            first_layer(e, 1)
            if e + 1 < E:
                gather_scales(e + 1)
                permute(e + 1)
            if 0 <= e - LAG < HOT:
                quantise(e - LAG)
            if e - 2 >= HOT:
                quantise(e - 2)
            if LAG <= e < E - 1:
                second_layer(e - LAG)
        for unit in range(E - 2, len(UNITS)):
            quantise(unit)
            second_layer(unit - 1)
        second_layer(len(UNITS) - 1)
